import numpy as np
import ml_dtypes


def mxq(x, axis, fmt="e4m3"):
    dtype, down = {"e4m3": (ml_dtypes.float8_e4m3fn, 7), "e5m2": (ml_dtypes.float8_e5m2, 14)}[fmt]
    v = np.moveaxis(np.asarray(x, np.float32).astype(ml_dtypes.bfloat16).astype(np.float64), axis, -1)
    blocks = v.reshape(v.shape[:-1] + (-1, 32))
    amax = np.abs(blocks).max(-1, keepdims=True)
    byte = np.maximum(np.where(amax > 0, np.frexp(amax)[1] - 1 + 127, 0) - down, 1)
    scale = np.exp2(byte - 127.0)
    codes = (blocks / scale).astype(np.float32).astype(dtype).astype(np.float64)
    return np.moveaxis((codes * scale).reshape(v.shape), -1, axis)


WIDE = False


def mx_kscale(k):
    if not WIDE:
        return np.ones(k)
    levels = np.array([10, -10, 5, -5, 0])
    if k % 512:
        return np.exp2(np.random.permutation(np.resize(levels, k // 32))).repeat(32)
    a = np.empty((k // 512, 16))
    for p in range(k // 512):
        a[p, :8] = np.random.permutation(np.resize(levels, 8))
        for g in range(8):
            far = levels[np.abs(levels - a[p, g]) >= 10]
            a[p, g + 8] = far[np.random.randint(len(far))]
    return np.exp2(a.ravel()).repeat(32)


def f64(x):
    return np.asarray(x).astype(np.float64)


def striped(idx):
    return np.tile(idx.reshape(-1, 16).T, (8, 1)).astype(np.uint16)


def unstriped(offs):
    return offs[:16].T.reshape(-1).astype(np.int64)


E2M1 = np.array([0.0, 0.5, 1.0, 1.5, 2.0, 3.0, 4.0, 6.0, -0.0, -0.5, -1.0, -1.5, -2.0, -3.0, -4.0, -6.0])


def pack_fp4(w):
    k, n = w.shape
    w = f64(np.asarray(w, np.float32).astype(ml_dtypes.bfloat16)).reshape(k // 32, 32, n)
    amax = np.abs(w).max(1)
    mant, ex = np.frexp(amax / 6.0)
    byte = np.clip(np.where(amax > 0, np.where(mant > 0.5, ex, ex - 1) + 127, 1), 1, 254)
    scaled = (w * np.exp2(127.0 - byte)[:, None, :]).reshape(k, n).astype(np.float32)
    c = np.ascontiguousarray(scaled.reshape(k // 512, 128, 4, n).transpose(0, 1, 3, 2)).astype(ml_dtypes.float4_e2m1fn).view(np.uint8) & 0xF
    words = (c[..., 0::2] | (c[..., 1::2] << 4)).reshape(k // 512, 128, 2 * n)
    return np.ascontiguousarray(words), np.ascontiguousarray(byte.astype(np.uint8).reshape(k // 512, 16, n))


def unpack_fp4(words, scales):
    g, _, n = scales.shape
    words = np.ascontiguousarray(words).reshape(g, 128, n, 2)
    nib = np.empty((g, 128, n, 4), np.uint8)
    nib[..., 0::2] = words & 0xF
    nib[..., 1::2] = words >> 4
    vals = E2M1[nib] * np.repeat(np.exp2(scales.astype(np.float64) - 127.0), 8, axis=1)[..., None]
    return vals.transpose(0, 1, 3, 2).reshape(g * 512, n)


K, T, S, N, U = 1024, 2048, 1024, 128, 2048


def setup_inputs():
    n = np.random.standard_normal
    s = mx_kscale(K)[:, None]
    packed_w1 = pack_fp4(n((K, N)) / np.sqrt(K) / s)
    return {
        "xT": (n((K, T)) * s).astype(np.float32),
        "mem": n((N, U)).astype(np.float32),
        "w1_words": packed_w1[0],
        "w1_scales": packed_w1[1],
        "offs": striped(np.random.permutation(T)[:S]),
        "slot": striped(np.random.permutation(U)[:S]),
    }


def reference(xT, mem, w1_words, w1_scales, offs, slot):
    xq = mxq(f64(xT)[:, unstriped(offs)], 0, "e4m3")
    y = unpack_fp4(w1_words, w1_scales).T @ xq
    out = f64(mem).copy()
    out[:, unstriped(slot)] = np.minimum(f64(mem)[:, unstriped(slot)], y)
    return out

@@ -1,0 +1,149 @@
+from contextlib import ExitStack
+
+import concourse.mybir as mybir
+
+K, T, S, N, U = 1024, 2048, 1024, 128, 2048
+FLOPS = 2 * K * S * N
+
+F32 = mybir.dt.float32
+BF16 = mybir.dt.bfloat16
+I32 = mybir.dt.int32
+U32 = mybir.dt.uint32
+U16 = mybir.dt.uint16
+U8 = mybir.dt.uint8
+FP8X4 = mybir.dt.float8_e4m3fn_x4
+FP4X4 = mybir.dt.float4_e2m1fn_x4
+COPY = mybir.ActivationFunctionType.Copy
+MIN = mybir.AluOpType.min
+
+P = 128
+PACK = 4
+K_PASS = P * PACK
+
+PAIR_CHUNKS = [
+    [(0, 1024, 0), (1024, 2048, 640)],
+    [(0, 1024, 0), (1024, 1536, 512), (1536, 2048, 320)],
+    [(0, 512, 0), (512, 1024, 0), (1024, 1536, 0), (1536, 2048, 192)],
+]
+ROW_CHUNKS = {2: [(0, 1024), (1024, 2048)], 3: [(0, 1024), (1024, 1536), (1536, 2048)]}
+PIECES = [(0, 256), (256, 512), (512, 1024)]
+
+
+def tile_picked_idxput_min_e_kernel(tc, xT, mem, w1_words, w1_scales, offs, slot, out):
+    nc = tc.nc
+    with ExitStack() as ctx:
+        keep = ctx.enter_context(tc.tile_pool(name="keep", bufs=1))
+        psum = ctx.enter_context(tc.psum_pool(name="psum", bufs=1))
+
+        offs_t = keep.tile([P, S // 16], U16, name="offs_t")
+        slot_t = keep.tile([P, S // 16], U16, name="slot_t")
+        w_codes = keep.tile([P, 2, 2 * N], U8, name="w_codes", align_bytes=64)
+        w_scales = keep.tile([P, 2, N], U8, name="w_scales", align_bytes=64)
+        store = keep.tile([P, U], F32, name="store")
+
+        def x_rows(z):
+            return xT[z * K_PASS : (z + 1) * K_PASS, :].rearrange("(p t) n -> p t n", t=PACK)
+
+        def entries(lst, a, b):
+            return lst[:, a // 16 : b // 16]
+
+        nc.gpsimd.memset(w_scales[:].rearrange("p z n -> p (z n)").bitcast(I32), 0)
+        for q in range(4):
+            nc.gpsimd.dma_start(
+                out=w_scales[32 * q : 32 * q + 4, :, :].bitcast(I32),
+                in_=w1_scales[:, 4 * q : 4 * q + 4, :].rearrange("z r n -> r z n").bitcast(I32),
+            )
+
+        def load_pair(i):
+            z, u = divmod(i, 2)
+            pair = keep.tile([P, 2 * T], BF16, name=f"pair{i}")
+            pair_v = pair[:].rearrange("p (n e) -> p n e", e=2)
+            for c0, c1, on_vector in PAIR_CHUNKS[i]:
+                raw = keep.tile([P, 2, c1 - c0], F32, name=f"raw{i}_{c0}")
+                nc.sync.dma_start(out=raw[:], in_=x_rows(z)[:, 2 * u : 2 * u + 2, c0:c1])
+                if i == 0 and c0 == 0:
+                    nc.sync.dma_start(offs_t[:], offs)
+                turned = raw[:].rearrange("p e n -> p n e")
+                cut = c1 - c0 - on_vector
+                if cut:
+                    nc.scalar.activation(pair_v[:, c0 : c0 + cut, :], turned[:, :cut, :], COPY)
+                if on_vector:
+                    nc.vector.tensor_copy(pair_v[:, c0 + cut : c1, :], turned[:, cut:, :])
+            return pair[:].bitcast(U32)
+
+        def gather_pair(dst, window, u, a, b):
+            words = dst[:].bitcast(U32).rearrange("p (n u) -> p n u", u=2)
+            nc.vector.tensor_copy(words[:, :, u], window.indirect(entries(offs_t, a, b)))
+
+        picked0 = keep.tile([P, PACK * S], BF16, name="picked0", align_bytes=64)
+        codes0 = keep.tile([P, S], U32, name="codes0", align_bytes=64)
+        scales0 = keep.tile([P, S], U8, name="scales0", align_bytes=64)
+        for u in range(2):
+            gather_pair(picked0, load_pair(u), u, 0, S)
+        nc.vector.quantize_mx(out=codes0[:].bitcast(FP8X4), scales=scales0[:], in_=picked0[:])
+
+        picked1 = [keep.tile([P, PACK * (b - a)], BF16, name=f"picked1_{a}", align_bytes=64) for a, b in PIECES]
+        window = load_pair(2)
+        nc.sync.dma_start(slot_t[:], slot)
+        nc.sync.dma_start(out=w_codes[:].bitcast(I32), in_=w1_words.rearrange("z p c -> p z c").bitcast(I32))
+        for i in (1, 2, 0):
+            gather_pair(picked1[i], window, 0, *PIECES[i])
+
+        def load_row(t):
+            row = keep.tile([P, T], F32, name=f"row{t}")
+            row16 = keep.tile([P, T], BF16, name=f"row16_{t}")
+            for c0, c1 in ROW_CHUNKS[t]:
+                nc.sync.dma_start(out=row[:, c0:c1], in_=x_rows(1)[:, t, c0:c1])
+                nc.scalar.activation(row16[:, c0:c1], row[:, c0:c1], COPY)
+            return row, row16
+
+        def gather_row(i, t, row, row16):
+            a, b = PIECES[i]
+            dst = picked1[i][:].rearrange("p (n t) -> p n t", t=PACK)[:, :, t]
+            if i == 0:
+                nc.vector.tensor_copy(dst, row[:].indirect(entries(offs_t, a, b)))
+            else:
+                nc.scalar.activation(dst, row16[:].indirect(entries(offs_t, a, b)), COPY)
+
+        row, row16 = load_row(2)
+        for i in range(len(PIECES)):
+            gather_row(i, 2, row, row16)
+
+        nc.sync.dma_start(out=store[:], in_=mem)
+        old = keep.tile([P, S], F32, name="old")
+        nc.vector.tensor_copy(old[:], store[:].indirect(slot_t[:]))
+
+        row, row16 = load_row(3)
+        for i in range(len(PIECES)):
+            gather_row(i, 3, row, row16)
+
+        def product(i):
+            a, b = PIECES[i]
+            n = b - a
+            codes1 = keep.tile([P, n], U32, name=f"codes1_{a}", tag="codes1", align_bytes=64)
+            scales1 = keep.tile([P, n], U8, name=f"scales1_{a}", align_bytes=64)
+            nc.vector.quantize_mx(out=codes1[:].bitcast(FP8X4), scales=scales1[:], in_=picked1[i][:])
+            acc = psum.tile([P, n], F32, name=f"acc{a}")
+            step = 512 if n == 512 else 128
+            for c in range(0, n, step):
+                for z, (codes, scales, first) in enumerate(((codes0, scales0, a + c), (codes1, scales1, c))):
+                    nc.tensor.matmul_mx(
+                        out=acc[:, c : c + step],
+                        lhsT=w_codes[:, z, :].bitcast(FP4X4),
+                        lhsT_scale=w_scales[:, z, :],
+                        rhs=codes[:, first : first + step].bitcast(FP8X4),
+                        rhs_scale=scales[:, first : first + step],
+                        start=(z == 0),
+                        stop=(z == 1),
+                    )
+            return acc
+
+        acc = product(0)
+        for i, (a, b) in enumerate(PIECES):
+            new = keep.tile([P, b - a], F32, name=f"new{a}")
+            nc.vector.tensor_tensor(new[:], acc[:], old[:, a:b], MIN)
+            if i + 1 < len(PIECES):
+                acc = product(i + 1)
+            nc.vector.tensor_copy(store[:].indirect(entries(slot_t, a, b)), new[:])
+
+        nc.sync.dma_start(out=out, in_=store[:])

@@ -22,11 +22,13 @@ K_PASS = P * PACK
 
 PAIR_CHUNKS = [
     [(0, 1024, 0), (1024, 2048, 640)],
-    [(0, 1024, 0), (1024, 1536, 512), (1536, 2048, 320)],
-    [(0, 512, 0), (512, 1024, 0), (1024, 1536, 0), (1536, 2048, 192)],
+    [(0, 1024, 0), (1024, 2048, 640)],
+    [(0, 512, 0), (512, 1024, 0), (1024, 1536, 0), (1536, 2048, 128)],
 ]
-ROW_CHUNKS = {2: [(0, 1024), (1024, 2048)], 3: [(0, 1024), (1024, 1536), (1536, 2048)]}
-PIECES = [(0, 256), (256, 512), (512, 1024)]
+ROW_CHUNKS = {2: [(0, 1024), (1024, 2048)], 3: [(0, 1024), (1024, 2048)]}
+PIECES = [(0, 256), (768, 1024), (256, 768)]
+GROUPS = [(0, 128), (128, 256), (768, 896), (896, 1024), (256, 768)]
+FRONT = 768
 
 
 def tile_picked_idxput_min_e_kernel(tc, xT, mem, w1_words, w1_scales, offs, slot, out):
@@ -46,13 +48,6 @@ def tile_picked_idxput_min_e_kernel(tc, xT, mem, w1_words, w1_scales, offs, slot
 
         def entries(lst, a, b):
             return lst[:, a // 16 : b // 16]
-
-        nc.gpsimd.memset(w_scales[:].rearrange("p z n -> p (z n)").bitcast(I32), 0)
-        for q in range(4):
-            nc.gpsimd.dma_start(
-                out=w_scales[32 * q : 32 * q + 4, :, :].bitcast(I32),
-                in_=w1_scales[:, 4 * q : 4 * q + 4, :].rearrange("z r n -> r z n").bitcast(I32),
-            )
 
         def load_pair(i):
             z, u = divmod(i, 2)
@@ -75,6 +70,20 @@ def tile_picked_idxput_min_e_kernel(tc, xT, mem, w1_words, w1_scales, offs, slot
             words = dst[:].bitcast(U32).rearrange("p (n u) -> p n u", u=2)
             nc.vector.tensor_copy(words[:, :, u], window.indirect(entries(offs_t, a, b)))
 
+        sums = [psum.tile([P, b - a], F32, name=f"sums{a}") for a, b in GROUPS]
+
+        def multiply(g, z, codes, scales, first):
+            a, b = GROUPS[g]
+            nc.tensor.matmul_mx(
+                out=sums[g][:],
+                lhsT=w_codes[:, z, :].bitcast(FP4X4),
+                lhsT_scale=w_scales[:, z, :],
+                rhs=codes[:, a - first : b - first].bitcast(FP8X4),
+                rhs_scale=scales[:, a - first : b - first],
+                start=(z == 0),
+                stop=(z == 1),
+            )
+
         picked0 = keep.tile([P, PACK * S], BF16, name="picked0", align_bytes=64)
         codes0 = keep.tile([P, S], U32, name="codes0", align_bytes=64)
         scales0 = keep.tile([P, S], U8, name="scales0", align_bytes=64)
@@ -84,9 +93,17 @@ def tile_picked_idxput_min_e_kernel(tc, xT, mem, w1_words, w1_scales, offs, slot
 
         picked1 = [keep.tile([P, PACK * (b - a)], BF16, name=f"picked1_{a}", align_bytes=64) for a, b in PIECES]
         window = load_pair(2)
-        nc.sync.dma_start(slot_t[:], slot)
         nc.sync.dma_start(out=w_codes[:].bitcast(I32), in_=w1_words.rearrange("z p c -> p z c").bitcast(I32))
-        for i in (1, 2, 0):
+        nc.vector.memset(w_scales[:].rearrange("p z n -> p (z n)").bitcast(I32), 0)
+        for q in range(4):
+            nc.sync.dma_start(
+                out=w_scales[32 * q : 32 * q + 4, :, :].bitcast(I32),
+                in_=w1_scales[:, 4 * q : 4 * q + 4, :].rearrange("z r n -> r z n").bitcast(I32),
+            )
+
+        for g in range(len(GROUPS)):
+            multiply(g, 0, codes0, scales0, 0)
+        for i in (0, 1, 2):
             gather_pair(picked1[i], window, 0, *PIECES[i])
 
         def load_row(t):
@@ -109,9 +126,10 @@ def tile_picked_idxput_min_e_kernel(tc, xT, mem, w1_words, w1_scales, offs, slot
         for i in range(len(PIECES)):
             gather_row(i, 2, row, row16)
 
+        nc.sync.dma_start(slot_t[:], slot)
         nc.sync.dma_start(out=store[:], in_=mem)
-        old = keep.tile([P, S], F32, name="old")
-        nc.vector.tensor_copy(old[:], store[:].indirect(slot_t[:]))
+        old_front = keep.tile([P, FRONT], F32, name="old_front")
+        nc.vector.tensor_copy(old_front[:], store[:].indirect(entries(slot_t, 0, FRONT)))
 
         row, row16 = load_row(3)
         for i in range(len(PIECES)):
@@ -119,31 +137,25 @@ def tile_picked_idxput_min_e_kernel(tc, xT, mem, w1_words, w1_scales, offs, slot
 
         def product(i):
             a, b = PIECES[i]
-            n = b - a
-            codes1 = keep.tile([P, n], U32, name=f"codes1_{a}", tag="codes1", align_bytes=64)
-            scales1 = keep.tile([P, n], U8, name=f"scales1_{a}", align_bytes=64)
+            codes1 = keep.tile([P, b - a], U32, name=f"codes1_{a}", tag="codes1", align_bytes=64)
+            scales1 = keep.tile([P, b - a], U8, name=f"scales1_{a}", align_bytes=64)
             nc.vector.quantize_mx(out=codes1[:].bitcast(FP8X4), scales=scales1[:], in_=picked1[i][:])
-            acc = psum.tile([P, n], F32, name=f"acc{a}")
-            step = 512 if n == 512 else 128
-            for c in range(0, n, step):
-                for z, (codes, scales, first) in enumerate(((codes0, scales0, a + c), (codes1, scales1, c))):
-                    nc.tensor.matmul_mx(
-                        out=acc[:, c : c + step],
-                        lhsT=w_codes[:, z, :].bitcast(FP4X4),
-                        lhsT_scale=w_scales[:, z, :],
-                        rhs=codes[:, first : first + step].bitcast(FP8X4),
-                        rhs_scale=scales[:, first : first + step],
-                        start=(z == 0),
-                        stop=(z == 1),
-                    )
-            return acc
+            for g, (c0, c1) in enumerate(GROUPS):
+                if a <= c0 < b:
+                    multiply(g, 1, codes1, scales1, a)
 
-        acc = product(0)
+        product(0)
+        old_back = keep.tile([P, S - FRONT], F32, name="old_back", tag="picked1_0", align_bytes=64)
+        nc.vector.tensor_copy(old_back[:], store[:].indirect(entries(slot_t, FRONT, S)))
         for i, (a, b) in enumerate(PIECES):
             new = keep.tile([P, b - a], F32, name=f"new{a}")
-            nc.vector.tensor_tensor(new[:], acc[:], old[:, a:b], MIN)
+            for g, (c0, c1) in enumerate(GROUPS):
+                if a <= c0 < b:
+                    old = old_front[:, c0:c1] if c1 <= FRONT else old_back[:, c0 - FRONT : c1 - FRONT]
+                    nc.vector.tensor_tensor(new[:, c0 - a : c1 - a], sums[g][:], old, MIN)
             if i + 1 < len(PIECES):
-                acc = product(i + 1)
+                product(i + 1)
             nc.vector.tensor_copy(store[:].indirect(entries(slot_t, a, b)), new[:])
 
-        nc.sync.dma_start(out=out, in_=store[:])
+        nc.sync.dma_start(out=out[:, : U // 2], in_=store[:, : U // 2])
+        nc.scalar.dma_start(out=out[:, U // 2 :], in_=store[:, U // 2 :])

@@ -25,10 +25,9 @@ PAIR_CHUNKS = [
     [(0, 1024, 0), (1024, 2048, 640)],
     [(0, 512, 0), (512, 1024, 0), (1024, 1536, 0), (1536, 2048, 128)],
 ]
-ROW_CHUNKS = {2: [(0, 1024), (1024, 2048)], 3: [(0, 1024), (1024, 2048)]}
-PIECES = [(0, 256), (768, 1024), (256, 768)]
-GROUPS = [(0, 128), (128, 256), (768, 896), (896, 1024), (256, 768)]
-FRONT = 768
+ROW_CHUNKS = {2: [(0, 1024, 0), (1024, 2048, 0)], 3: [(0, 1024, 512), (1024, 2048, 640)]}
+PIECES = [(0, 256), (256, 512), (512, 1024)]
+GROUPS = [(0, 512), (512, 1024)]
 
 
 def tile_picked_idxput_min_e_kernel(tc, xT, mem, w1_words, w1_scales, offs, slot, out):
@@ -87,75 +86,90 @@ def tile_picked_idxput_min_e_kernel(tc, xT, mem, w1_words, w1_scales, offs, slot
         picked0 = keep.tile([P, PACK * S], BF16, name="picked0", align_bytes=64)
         codes0 = keep.tile([P, S], U32, name="codes0", align_bytes=64)
         scales0 = keep.tile([P, S], U8, name="scales0", align_bytes=64)
-        for u in range(2):
-            gather_pair(picked0, load_pair(u), u, 0, S)
-        nc.vector.quantize_mx(out=codes0[:].bitcast(FP8X4), scales=scales0[:], in_=picked0[:])
-
-        picked1 = [keep.tile([P, PACK * (b - a)], BF16, name=f"picked1_{a}", align_bytes=64) for a, b in PIECES]
-        window = load_pair(2)
-        nc.sync.dma_start(out=w_codes[:].bitcast(I32), in_=w1_words.rearrange("z p c -> p z c").bitcast(I32))
+        gather_pair(picked0, load_pair(0), 0, 0, S)
         nc.vector.memset(w_scales[:].rearrange("p z n -> p (z n)").bitcast(I32), 0)
         for q in range(4):
             nc.sync.dma_start(
                 out=w_scales[32 * q : 32 * q + 4, :, :].bitcast(I32),
                 in_=w1_scales[:, 4 * q : 4 * q + 4, :].rearrange("z r n -> r z n").bitcast(I32),
             )
+        gather_pair(picked0, load_pair(1), 1, 0, S)
+        nc.vector.quantize_mx(out=codes0[:].bitcast(FP8X4), scales=scales0[:], in_=picked0[:])
 
+        picked1 = [keep.tile([P, PACK * (b - a)], BF16, name=f"picked1_{a}", align_bytes=64) for a, b in GROUPS]
+        window = load_pair(2)
         for g in range(len(GROUPS)):
-            multiply(g, 0, codes0, scales0, 0)
-        for i in (0, 1, 2):
-            gather_pair(picked1[i], window, 0, *PIECES[i])
+            gather_pair(picked1[g], window, 0, *GROUPS[g])
+
+        rows16 = keep.tile([P, 2 * T], BF16, name="rows16")
 
         def load_row(t):
             row = keep.tile([P, T], F32, name=f"row{t}")
-            row16 = keep.tile([P, T], BF16, name=f"row16_{t}")
-            for c0, c1 in ROW_CHUNKS[t]:
+            for c0, c1, on_vector in ROW_CHUNKS[t]:
                 nc.sync.dma_start(out=row[:, c0:c1], in_=x_rows(1)[:, t, c0:c1])
-                nc.scalar.activation(row16[:, c0:c1], row[:, c0:c1], COPY)
-            return row, row16
+                cut = c1 - on_vector
+                base = (t - 2) * T
+                nc.scalar.activation(rows16[:, base + c0 : base + cut], row[:, c0:cut], COPY)
+                if on_vector:
+                    nc.vector.tensor_copy(rows16[:, base + cut : base + c1], row[:, cut:c1])
+            return row
 
-        def gather_row(i, t, row, row16):
+        def gather_row(i, t, window):
             a, b = PIECES[i]
-            dst = picked1[i][:].rearrange("p (n t) -> p n t", t=PACK)[:, :, t]
+            g, first = divmod(a, S // 2)
+            dst = picked1[g][:].rearrange("p (n t) -> p n t", t=PACK)[:, first : first + b - a, t]
             if i == 0:
-                nc.vector.tensor_copy(dst, row[:].indirect(entries(offs_t, a, b)))
+                nc.vector.tensor_copy(dst, window.indirect(entries(offs_t, a, b)))
             else:
-                nc.scalar.activation(dst, row16[:].indirect(entries(offs_t, a, b)), COPY)
+                nc.scalar.activation(dst, window.indirect(entries(offs_t, a, b)), COPY)
 
-        row, row16 = load_row(2)
-        for i in range(len(PIECES)):
-            gather_row(i, 2, row, row16)
+        row = load_row(2)
+        gather_row(0, 2, row[:])
+        gather_row(1, 2, rows16[:, :T])
+        row = load_row(3)
+        gather_row(0, 3, row[:])
+        gather_row(1, 3, rows16[:, T:])
+        gather_row(2, 2, rows16[:])
+        gather_row(2, 3, rows16[:, T:])
 
+        nc.sync.dma_start(out=w_codes[:].bitcast(I32), in_=w1_words.rearrange("z p c -> p z c").bitcast(I32))
         nc.sync.dma_start(slot_t[:], slot)
         nc.sync.dma_start(out=store[:], in_=mem)
-        old_front = keep.tile([P, FRONT], F32, name="old_front")
-        nc.vector.tensor_copy(old_front[:], store[:].indirect(entries(slot_t, 0, FRONT)))
 
-        row, row16 = load_row(3)
-        for i in range(len(PIECES)):
-            gather_row(i, 3, row, row16)
+        for g in range(len(GROUPS)):
+            multiply(g, 0, codes0, scales0, 0)
 
-        def product(i):
-            a, b = PIECES[i]
-            codes1 = keep.tile([P, b - a], U32, name=f"codes1_{a}", tag="codes1", align_bytes=64)
+        def product(g, tag):
+            a, b = GROUPS[g]
+            codes1 = keep.tile([P, b - a], U32, name=f"codes1_{a}", tag=tag, align_bytes=64)
             scales1 = keep.tile([P, b - a], U8, name=f"scales1_{a}", align_bytes=64)
-            nc.vector.quantize_mx(out=codes1[:].bitcast(FP8X4), scales=scales1[:], in_=picked1[i][:])
-            for g, (c0, c1) in enumerate(GROUPS):
-                if a <= c0 < b:
-                    multiply(g, 1, codes1, scales1, a)
+            nc.vector.quantize_mx(out=codes1[:].bitcast(FP8X4), scales=scales1[:], in_=picked1[g][:])
+            multiply(g, 1, codes1, scales1, a)
 
-        product(0)
-        old_back = keep.tile([P, S - FRONT], F32, name="old_back", tag="picked1_0", align_bytes=64)
-        nc.vector.tensor_copy(old_back[:], store[:].indirect(entries(slot_t, FRONT, S)))
-        for i, (a, b) in enumerate(PIECES):
-            new = keep.tile([P, b - a], F32, name=f"new{a}")
-            for g, (c0, c1) in enumerate(GROUPS):
-                if a <= c0 < b:
-                    old = old_front[:, c0:c1] if c1 <= FRONT else old_back[:, c0 - FRONT : c1 - FRONT]
-                    nc.vector.tensor_tensor(new[:, c0 - a : c1 - a], sums[g][:], old, MIN)
-            if i + 1 < len(PIECES):
-                product(i + 1)
-            nc.vector.tensor_copy(store[:].indirect(entries(slot_t, a, b)), new[:])
+        def look_up(i):
+            a, b = PIECES[i]
+            old = keep.tile([P, b - a], F32, name=f"old{i}", tag=f"old{i}", align_bytes=64)
+            nc.vector.tensor_copy(old[:], store[:].indirect(entries(slot_t, a, b)))
+            return old
+
+        new = [keep.tile([P, b - a], F32, name=f"new{a}") for a, b in GROUPS]
+
+        def smaller(i, old):
+            a, b = PIECES[i]
+            g, first = divmod(a, S // 2)
+            nc.vector.tensor_tensor(new[g][:, first : first + b - a], sums[g][:, first : first + b - a], old[:], MIN)
+
+        def put(g):
+            nc.vector.tensor_copy(store[:].indirect(entries(slot_t, *GROUPS[g])), new[g][:])
+
+        product(0, "codes1_0")
+        old = [look_up(i) for i in range(len(PIECES))]
+        smaller(0, old[0])
+        smaller(1, old[1])
+        product(1, "old0")
+        put(0)
+        smaller(2, old[2])
+        put(1)
 
         nc.sync.dma_start(out=out[:, : U // 2], in_=store[:, : U // 2])
         nc.scalar.dma_start(out=out[:, U // 2 :], in_=store[:, U // 2 :])

@@ -23,7 +23,7 @@ K_PASS = P * PACK
 PAIR_CHUNKS = [
     [(0, 1024, 0), (1024, 2048, 640)],
     [(0, 1024, 0), (1024, 2048, 640)],
-    [(0, 512, 0), (512, 1024, 0), (1024, 1536, 0), (1536, 2048, 128)],
+    [(0, 512, 0), (512, 1024, 0), (1024, 1536, 0), (1536, 2048, 256)],
 ]
 ROW_CHUNKS = {2: [(0, 1024, 0), (1024, 2048, 0)], 3: [(0, 1024, 512), (1024, 2048, 640)]}
 PIECES = [(0, 256), (256, 512), (512, 1024)]
@@ -152,24 +152,25 @@ def tile_picked_idxput_min_e_kernel(tc, xT, mem, w1_words, w1_scales, offs, slot
             nc.vector.tensor_copy(old[:], store[:].indirect(entries(slot_t, a, b)))
             return old
 
-        new = [keep.tile([P, b - a], F32, name=f"new{a}") for a, b in GROUPS]
+        new = [keep.tile([P, b - a], F32, name=f"new{a}") for a, b in PIECES]
 
         def smaller(i, old):
             a, b = PIECES[i]
             g, first = divmod(a, S // 2)
-            nc.vector.tensor_tensor(new[g][:, first : first + b - a], sums[g][:, first : first + b - a], old[:], MIN)
+            nc.vector.tensor_tensor(new[i][:], sums[g][:, first : first + b - a], old[:], MIN)
 
-        def put(g):
-            nc.vector.tensor_copy(store[:].indirect(entries(slot_t, *GROUPS[g])), new[g][:])
+        def put(i):
+            nc.vector.tensor_copy(store[:].indirect(entries(slot_t, *PIECES[i])), new[i][:])
 
         product(0, "codes1_0")
         old = [look_up(i) for i in range(len(PIECES))]
         smaller(0, old[0])
         smaller(1, old[1])
-        product(1, "old0")
         put(0)
-        smaller(2, old[2])
+        product(1, "old1")
         put(1)
+        smaller(2, old[2])
+        put(2)
 
         nc.sync.dma_start(out=out[:, : U // 2], in_=store[:, : U // 2])
         nc.scalar.dma_start(out=out[:, U // 2 :], in_=store[:, U // 2 :])

@@ -15,6 +15,8 @@ FP8X4 = mybir.dt.float8_e4m3fn_x4
 FP4X4 = mybir.dt.float4_e2m1fn_x4
 COPY = mybir.ActivationFunctionType.Copy
 MIN = mybir.AluOpType.min
+MULT = mybir.AluOpType.mult
+ADD = mybir.AluOpType.add
 
 P = 128
 PACK = 4
@@ -25,7 +27,7 @@ PAIR_CHUNKS = [
     [(0, 1024, 0), (1024, 2048, 640)],
     [(0, 512, 0), (512, 1024, 0), (1024, 1536, 0), (1536, 2048, 256)],
 ]
-ROW_CHUNKS = {2: [(0, 1024, 0), (1024, 2048, 0)], 3: [(0, 1024, 512), (1024, 2048, 640)]}
+ROW_CHUNKS = {2: [(0, 1024, 1024), (1024, 2048, 448)], 3: [(0, 1024, 640), (1024, 2048, 448)]}
 PIECES = [(0, 256), (256, 512), (512, 1024)]
 GROUPS = [(0, 512), (512, 1024)]
 
@@ -109,9 +111,9 @@ def tile_picked_idxput_min_e_kernel(tc, xT, mem, w1_words, w1_scales, offs, slot
                 nc.sync.dma_start(out=row[:, c0:c1], in_=x_rows(1)[:, t, c0:c1])
                 cut = c1 - on_vector
                 base = (t - 2) * T
-                nc.scalar.activation(rows16[:, base + c0 : base + cut], row[:, c0:cut], COPY)
-                if on_vector:
-                    nc.vector.tensor_copy(rows16[:, base + cut : base + c1], row[:, cut:c1])
+                if cut > c0:
+                    nc.scalar.activation(rows16[:, base + c0 : base + cut], row[:, c0:cut], COPY)
+                nc.gpsimd.tensor_scalar(rows16[:, base + cut : base + c1], row[:, cut:c1], 1.0, 0.0, MULT, ADD)
             return row
 
         def gather_row(i, t, window):

@@ -85,18 +85,18 @@ def tile_picked_idxput_min_e_kernel(tc, xT, mem, w1_words, w1_scales, offs, slot
                 stop=(z == 1),
             )
 
-        picked0 = keep.tile([P, PACK * S], BF16, name="picked0", align_bytes=64)
-        codes0 = keep.tile([P, S], U32, name="codes0", align_bytes=64)
-        scales0 = keep.tile([P, S], U8, name="scales0", align_bytes=64)
-        gather_pair(picked0, load_pair(0), 0, 0, S)
+        picked0 = [keep.tile([P, PACK * (b - a)], BF16, name=f"picked0_{a}", align_bytes=64) for a, b in GROUPS]
+        codes0 = [keep.tile([P, b - a], U32, name=f"codes0_{a}", align_bytes=64) for a, b in GROUPS]
+        scales0 = [keep.tile([P, b - a], U8, name=f"scales0_{a}", align_bytes=64) for a, b in GROUPS]
+        window = load_pair(0)
+        for g in range(len(GROUPS)):
+            gather_pair(picked0[g], window, 0, *GROUPS[g])
         nc.vector.memset(w_scales[:].rearrange("p z n -> p (z n)").bitcast(I32), 0)
-        for q in range(4):
-            nc.sync.dma_start(
-                out=w_scales[32 * q : 32 * q + 4, :, :].bitcast(I32),
-                in_=w1_scales[:, 4 * q : 4 * q + 4, :].rearrange("z r n -> r z n").bitcast(I32),
-            )
-        gather_pair(picked0, load_pair(1), 1, 0, S)
-        nc.vector.quantize_mx(out=codes0[:].bitcast(FP8X4), scales=scales0[:], in_=picked0[:])
+        window = load_pair(1)
+        for g in range(len(GROUPS)):
+            gather_pair(picked0[g], window, 1, *GROUPS[g])
+        for g in range(len(GROUPS)):
+            nc.vector.quantize_mx(out=codes0[g][:].bitcast(FP8X4), scales=scales0[g][:], in_=picked0[g][:])
 
         picked1 = [keep.tile([P, PACK * (b - a)], BF16, name=f"picked1_{a}", align_bytes=64) for a, b in GROUPS]
         window = load_pair(2)
@@ -134,18 +134,21 @@ def tile_picked_idxput_min_e_kernel(tc, xT, mem, w1_words, w1_scales, offs, slot
         gather_row(2, 2, rows16[:])
         gather_row(2, 3, rows16[:, T:])
 
-        nc.sync.dma_start(out=w_codes[:].bitcast(I32), in_=w1_words.rearrange("z p c -> p z c").bitcast(I32))
         nc.sync.dma_start(slot_t[:], slot)
         nc.sync.dma_start(out=store[:], in_=mem)
-
-        for g in range(len(GROUPS)):
-            multiply(g, 0, codes0, scales0, 0)
+        nc.sync.dma_start(out=w_codes[:].bitcast(I32), in_=w1_words.rearrange("z p c -> p z c").bitcast(I32))
+        for q in range(4):
+            nc.sync.dma_start(
+                out=w_scales[32 * q : 32 * q + 4, :, :].bitcast(I32),
+                in_=w1_scales[:, 4 * q : 4 * q + 4, :].rearrange("z r n -> r z n").bitcast(I32),
+            )
 
         def product(g, tag):
             a, b = GROUPS[g]
             codes1 = keep.tile([P, b - a], U32, name=f"codes1_{a}", tag=tag, align_bytes=64)
             scales1 = keep.tile([P, b - a], U8, name=f"scales1_{a}", align_bytes=64)
             nc.vector.quantize_mx(out=codes1[:].bitcast(FP8X4), scales=scales1[:], in_=picked1[g][:])
+            multiply(g, 0, codes0[g], scales0[g], a)
             multiply(g, 1, codes1, scales1, a)
 
         def look_up(i):

@@ -23,11 +23,11 @@ PACK = 4
 K_PASS = P * PACK
 
 PAIR_CHUNKS = [
-    [(0, 1024, 0), (1024, 2048, 640)],
-    [(0, 1024, 0), (1024, 2048, 640)],
-    [(0, 512, 0), (512, 1024, 0), (1024, 1536, 0), (1536, 2048, 256)],
+    [(0, 1280, 768, 0), (1280, 2048, 512, 0)],
+    [(0, 1280, 0, 576), (1280, 2048, 512, 0)],
+    [(0, 768, 0, 352), (768, 1536, 0, 192), (1536, 2048, 256, 0)],
 ]
-ROW_CHUNKS = {2: [(0, 1024, 1024), (1024, 2048, 448)], 3: [(0, 1024, 640), (1024, 2048, 448)]}
+ROW_CHUNKS = {2: [(0, 1280, 768), (1280, 2048, 352)], 3: [(0, 1280, 640), (1280, 2048, 352)]}
 PIECES = [(0, 256), (256, 512), (512, 1024)]
 GROUPS = [(0, 512), (512, 1024)]
 
@@ -54,17 +54,20 @@ def tile_picked_idxput_min_e_kernel(tc, xT, mem, w1_words, w1_scales, offs, slot
             z, u = divmod(i, 2)
             pair = keep.tile([P, 2 * T], BF16, name=f"pair{i}")
             pair_v = pair[:].rearrange("p (n e) -> p n e", e=2)
-            for c0, c1, on_vector in PAIR_CHUNKS[i]:
+            for c0, c1, on_vector, on_gpsimd in PAIR_CHUNKS[i]:
                 raw = keep.tile([P, 2, c1 - c0], F32, name=f"raw{i}_{c0}")
                 nc.sync.dma_start(out=raw[:], in_=x_rows(z)[:, 2 * u : 2 * u + 2, c0:c1])
                 if i == 0 and c0 == 0:
                     nc.sync.dma_start(offs_t[:], offs)
                 turned = raw[:].rearrange("p e n -> p n e")
-                cut = c1 - c0 - on_vector
+                end = c1 - c0 - on_vector
+                cut = end - on_gpsimd
                 if cut:
                     nc.scalar.activation(pair_v[:, c0 : c0 + cut, :], turned[:, :cut, :], COPY)
+                if on_gpsimd:
+                    nc.gpsimd.tensor_scalar(pair_v[:, c0 + cut : c0 + end, :], turned[:, cut:end, :], 1.0, 0.0, MULT, ADD)
                 if on_vector:
-                    nc.vector.tensor_copy(pair_v[:, c0 + cut : c1, :], turned[:, cut:, :])
+                    nc.vector.tensor_copy(pair_v[:, c0 + end : c1, :], turned[:, end:, :])
             return pair[:].bitcast(U32)
 
         def gather_pair(dst, window, u, a, b):
@@ -98,18 +101,18 @@ def tile_picked_idxput_min_e_kernel(tc, xT, mem, w1_words, w1_scales, offs, slot
         for g in range(len(GROUPS)):
             nc.vector.quantize_mx(out=codes0[g][:].bitcast(FP8X4), scales=scales0[g][:], in_=picked0[g][:])
 
-        picked1 = [keep.tile([P, PACK * (b - a)], BF16, name=f"picked1_{a}", align_bytes=64) for a, b in GROUPS]
+        picked1 = [keep.tile([P, PACK * (b - a)], BF16, name=f"picked1_{a}", align_bytes=64) for a, b in PIECES]
         window = load_pair(2)
-        for g in range(len(GROUPS)):
-            gather_pair(picked1[g], window, 0, *GROUPS[g])
+        for i in range(len(PIECES)):
+            gather_pair(picked1[i], window, 0, *PIECES[i])
 
         rows16 = keep.tile([P, 2 * T], BF16, name="rows16")
 
         def load_row(t):
             row = keep.tile([P, T], F32, name=f"row{t}")
-            for c0, c1, on_vector in ROW_CHUNKS[t]:
+            for c0, c1, on_gpsimd in ROW_CHUNKS[t]:
                 nc.sync.dma_start(out=row[:, c0:c1], in_=x_rows(1)[:, t, c0:c1])
-                cut = c1 - on_vector
+                cut = c1 - on_gpsimd
                 base = (t - 2) * T
                 if cut > c0:
                     nc.scalar.activation(rows16[:, base + c0 : base + cut], row[:, c0:cut], COPY)
@@ -118,8 +121,7 @@ def tile_picked_idxput_min_e_kernel(tc, xT, mem, w1_words, w1_scales, offs, slot
 
         def gather_row(i, t, window):
             a, b = PIECES[i]
-            g, first = divmod(a, S // 2)
-            dst = picked1[g][:].rearrange("p (n t) -> p n t", t=PACK)[:, first : first + b - a, t]
+            dst = picked1[i][:].rearrange("p (n t) -> p n t", t=PACK)[:, :, t]
             if i == 0:
                 nc.vector.tensor_copy(dst, window.indirect(entries(offs_t, a, b)))
             else:
@@ -147,7 +149,9 @@ def tile_picked_idxput_min_e_kernel(tc, xT, mem, w1_words, w1_scales, offs, slot
             a, b = GROUPS[g]
             codes1 = keep.tile([P, b - a], U32, name=f"codes1_{a}", tag=tag, align_bytes=64)
             scales1 = keep.tile([P, b - a], U8, name=f"scales1_{a}", align_bytes=64)
-            nc.vector.quantize_mx(out=codes1[:].bitcast(FP8X4), scales=scales1[:], in_=picked1[g][:])
+            for i, (c, d) in enumerate(PIECES):
+                if a <= c < b:
+                    nc.vector.quantize_mx(out=codes1[:, c - a : d - a].bitcast(FP8X4), scales=scales1[:, c - a : d - a], in_=picked1[i][:])
             multiply(g, 0, codes0[g], scales0[g], a)
             multiply(g, 1, codes1, scales1, a)
 

@@ -23,11 +23,11 @@ PACK = 4
 K_PASS = P * PACK
 
 PAIR_CHUNKS = [
-    [(0, 1280, 768, 0), (1280, 2048, 512, 0)],
-    [(0, 1280, 0, 576), (1280, 2048, 512, 0)],
-    [(0, 768, 0, 352), (768, 1536, 0, 192), (1536, 2048, 256, 0)],
+    [(0, 1024, 0, 0), (1024, 2048, 640, 0)],
+    [(0, 1024, 0, 0), (1024, 1536, 256, 0), (1536, 2048, 352, 0)],
+    [(0, 512, 0, 0), (512, 1024, 0, 0), (1024, 1536, 0, 0), (1536, 2048, 256, 0)],
 ]
-ROW_CHUNKS = {2: [(0, 1280, 768), (1280, 2048, 352)], 3: [(0, 1280, 640), (1280, 2048, 352)]}
+ROW_CHUNKS = {2: [(0, 1024, 1024), (1024, 2048, 448)], 3: [(0, 1024, 704), (1024, 1536, 256), (1536, 2048, 224)]}
 PIECES = [(0, 256), (256, 512), (512, 1024)]
 GROUPS = [(0, 512), (512, 1024)]
 
@@ -155,30 +155,30 @@ def tile_picked_idxput_min_e_kernel(tc, xT, mem, w1_words, w1_scales, offs, slot
             multiply(g, 0, codes0[g], scales0[g], a)
             multiply(g, 1, codes1, scales1, a)
 
-        def look_up(i):
-            a, b = PIECES[i]
-            old = keep.tile([P, b - a], F32, name=f"old{i}", tag=f"old{i}", align_bytes=64)
+        def look_up(g):
+            a, b = GROUPS[g]
+            old = keep.tile([P, b - a], F32, name=f"old{g}", tag=f"old{g}", align_bytes=64)
             nc.vector.tensor_copy(old[:], store[:].indirect(entries(slot_t, a, b)))
             return old
 
         new = [keep.tile([P, b - a], F32, name=f"new{a}") for a, b in PIECES]
 
-        def smaller(i, old):
+        def smaller(i):
             a, b = PIECES[i]
             g, first = divmod(a, S // 2)
-            nc.vector.tensor_tensor(new[i][:], sums[g][:, first : first + b - a], old[:], MIN)
+            nc.vector.tensor_tensor(new[i][:], sums[g][:, first : first + b - a], old[g][:, first : first + b - a], MIN)
 
         def put(i):
             nc.vector.tensor_copy(store[:].indirect(entries(slot_t, *PIECES[i])), new[i][:])
 
         product(0, "codes1_0")
-        old = [look_up(i) for i in range(len(PIECES))]
-        smaller(0, old[0])
-        smaller(1, old[1])
+        old = [look_up(g) for g in range(len(GROUPS))]
+        smaller(0)
+        smaller(1)
         put(0)
-        product(1, "old1")
+        product(1, "old0")
         put(1)
-        smaller(2, old[2])
+        smaller(2)
         put(2)
 
         nc.sync.dma_start(out=out[:, : U // 2], in_=store[:, : U // 2])

@@ -23,9 +23,9 @@ PACK = 4
 K_PASS = P * PACK
 
 PAIR_CHUNKS = [
-    [(0, 1024, 0, 0), (1024, 2048, 640, 0)],
-    [(0, 1024, 0, 0), (1024, 1536, 256, 0), (1536, 2048, 352, 0)],
-    [(0, 512, 0, 0), (512, 1024, 0, 0), (1024, 1536, 0, 0), (1536, 2048, 256, 0)],
+    [(0, 2048, 1344, 0)],
+    [(0, 1024, 0, 0), (1024, 2048, 576, 0)],
+    [(0, 1024, 0, 512), (1024, 1536, 0, 0), (1536, 2048, 0, 0)],
 ]
 ROW_CHUNKS = {2: [(0, 1024, 1024), (1024, 2048, 448)], 3: [(0, 1024, 704), (1024, 1536, 256), (1536, 2048, 224)]}
 PIECES = [(0, 256), (256, 512), (512, 1024)]

@@ -24,10 +24,10 @@ K_PASS = P * PACK
 
 PAIR_CHUNKS = [
     [(0, 2048, 1344, 0)],
-    [(0, 1024, 0, 0), (1024, 2048, 576, 0)],
-    [(0, 1024, 0, 512), (1024, 1536, 0, 0), (1536, 2048, 0, 0)],
+    [(0, 2048, 1344, 0)],
+    [(0, 1024, 0, 768), (1024, 2048, 320, 0)],
 ]
-ROW_CHUNKS = {2: [(0, 1024, 1024), (1024, 2048, 448)], 3: [(0, 1024, 704), (1024, 1536, 256), (1536, 2048, 224)]}
+ROW_CHUNKS = {2: [(0, 2048, 1024)], 3: [(0, 1024, 1024), (1024, 2048, 448)]}
 PIECES = [(0, 256), (256, 512), (512, 1024)]
 GROUPS = [(0, 512), (512, 1024)]
 
@@ -74,6 +74,14 @@ def tile_picked_idxput_min_e_kernel(tc, xT, mem, w1_words, w1_scales, offs, slot
             words = dst[:].bitcast(U32).rearrange("p (n u) -> p n u", u=2)
             nc.vector.tensor_copy(words[:, :, u], window.indirect(entries(offs_t, a, b)))
 
+        def gather_flat(dst, window, u, a, b):
+            words = dst[:].bitcast(U32)
+            nc.vector.tensor_copy(words[:, u * (b - a) : (u + 1) * (b - a)], window.indirect(entries(offs_t, a, b)))
+
+        def weave(dst, src):
+            words = dst[:].bitcast(U32).rearrange("p (n u) -> p n u", u=2)
+            nc.scalar.copy(words, src[:].bitcast(U32).rearrange("p (u n) -> p n u", u=2))
+
         sums = [psum.tile([P, b - a], F32, name=f"sums{a}") for a, b in GROUPS]
 
         def multiply(g, z, codes, scales, first):
@@ -89,22 +97,26 @@ def tile_picked_idxput_min_e_kernel(tc, xT, mem, w1_words, w1_scales, offs, slot
             )
 
         picked0 = [keep.tile([P, PACK * (b - a)], BF16, name=f"picked0_{a}", align_bytes=64) for a, b in GROUPS]
-        codes0 = [keep.tile([P, b - a], U32, name=f"codes0_{a}", align_bytes=64) for a, b in GROUPS]
+        flat0 = keep.tile([P, PACK * 512], BF16, name="flat0", tag="flat0", align_bytes=64)
         scales0 = [keep.tile([P, b - a], U8, name=f"scales0_{a}", align_bytes=64) for a, b in GROUPS]
         window = load_pair(0)
-        for g in range(len(GROUPS)):
-            gather_pair(picked0[g], window, 0, *GROUPS[g])
+        gather_flat(flat0, window, 0, *GROUPS[1])
+        gather_pair(picked0[0], window, 0, *GROUPS[0])
         nc.vector.memset(w_scales[:].rearrange("p z n -> p (z n)").bitcast(I32), 0)
         window = load_pair(1)
-        for g in range(len(GROUPS)):
-            gather_pair(picked0[g], window, 1, *GROUPS[g])
-        for g in range(len(GROUPS)):
+        gather_flat(flat0, window, 1, *GROUPS[1])
+        gather_pair(picked0[0], window, 1, *GROUPS[0])
+        weave(picked0[1], flat0)
+        codes0 = [keep.tile([P, 512], U32, name=f"codes0_{g}", tag=tag, align_bytes=64) for g, tag in enumerate(("flat0", "codes0_1"))]
+        for g in (1, 0):
             nc.vector.quantize_mx(out=codes0[g][:].bitcast(FP8X4), scales=scales0[g][:], in_=picked0[g][:])
 
         picked1 = [keep.tile([P, PACK * (b - a)], BF16, name=f"picked1_{a}", align_bytes=64) for a, b in PIECES]
         window = load_pair(2)
-        for i in range(len(PIECES)):
+        flat1 = keep.tile([P, PACK * 512], BF16, name="flat1", align_bytes=64)
+        for i in range(2):
             gather_pair(picked1[i], window, 0, *PIECES[i])
+        gather_flat(flat1, window, 0, *PIECES[2])
 
         rows16 = keep.tile([P, 2 * T], BF16, name="rows16")
 
@@ -121,7 +133,10 @@ def tile_picked_idxput_min_e_kernel(tc, xT, mem, w1_words, w1_scales, offs, slot
 
         def gather_row(i, t, window):
             a, b = PIECES[i]
-            dst = picked1[i][:].rearrange("p (n t) -> p n t", t=PACK)[:, :, t]
+            if i == 2:
+                dst = flat1[:, 2 * (b - a) :].rearrange("p (n e) -> p n e", e=2)[:, :, t - 2]
+            else:
+                dst = picked1[i][:].rearrange("p (n t) -> p n t", t=PACK)[:, :, t]
             if i == 0:
                 nc.vector.tensor_copy(dst, window.indirect(entries(offs_t, a, b)))
             else:
@@ -135,6 +150,7 @@ def tile_picked_idxput_min_e_kernel(tc, xT, mem, w1_words, w1_scales, offs, slot
         gather_row(1, 3, rows16[:, T:])
         gather_row(2, 2, rows16[:])
         gather_row(2, 3, rows16[:, T:])
+        weave(picked1[2], flat1)
 
         nc.sync.dma_start(slot_t[:], slot)
         nc.sync.dma_start(out=store[:], in_=mem)

@@ -24,8 +24,8 @@ K_PASS = P * PACK
 
 PAIR_CHUNKS = [
     [(0, 2048, 1344, 0)],
-    [(0, 2048, 1344, 0)],
-    [(0, 1024, 0, 768), (1024, 2048, 320, 0)],
+    [(0, 1024, 0, 448), (1024, 2048, 672, 0)],
+    [(0, 1024, 0, 512), (1024, 2048, 512, 0)],
 ]
 ROW_CHUNKS = {2: [(0, 2048, 1024)], 3: [(0, 1024, 1024), (1024, 2048, 448)]}
 PIECES = [(0, 256), (256, 512), (512, 1024)]

@@ -55,11 +55,19 @@ def tile_picked_idxput_min_e_kernel(tc, xT, mem, w1_words, w1_scales, offs, slot
             pair = keep.tile([P, 2 * T], BF16, name=f"pair{i}")
             pair_v = pair[:].rearrange("p (n e) -> p n e", e=2)
             for c0, c1, on_vector, on_gpsimd in PAIR_CHUNKS[i]:
-                raw = keep.tile([P, 2, c1 - c0], F32, name=f"raw{i}_{c0}")
-                nc.sync.dma_start(out=raw[:], in_=x_rows(z)[:, 2 * u : 2 * u + 2, c0:c1])
+                if i == 1:
+                    if c0 == 0:
+                        both = keep.tile([P, 2 * T], F32, name="raw1")
+                    run = x_rows(z)[:, 2 * u : 2 * u + 2, :].rearrange("p e n -> p (e n)")
+                    first = 0 if c0 == 0 else T + c0
+                    nc.sync.dma_start(out=both[:, first : T + c1], in_=run[:, first : T + c1])
+                    turned = both[:].rearrange("p (e n) -> p n e", e=2)[:, c0:c1, :]
+                else:
+                    raw = keep.tile([P, 2, c1 - c0], F32, name=f"raw{i}_{c0}")
+                    nc.sync.dma_start(out=raw[:], in_=x_rows(z)[:, 2 * u : 2 * u + 2, c0:c1])
+                    turned = raw[:].rearrange("p e n -> p n e")
                 if i == 0 and c0 == 0:
                     nc.sync.dma_start(offs_t[:], offs)
-                turned = raw[:].rearrange("p e n -> p n e")
                 end = c1 - c0 - on_vector
                 cut = end - on_gpsimd
                 if cut:
@@ -82,12 +90,11 @@ def tile_picked_idxput_min_e_kernel(tc, xT, mem, w1_words, w1_scales, offs, slot
             words = dst[:].bitcast(U32).rearrange("p (n u) -> p n u", u=2)
             nc.scalar.copy(words, src[:].bitcast(U32).rearrange("p (u n) -> p n u", u=2))
 
-        sums = [psum.tile([P, b - a], F32, name=f"sums{a}") for a, b in GROUPS]
+        sums = [psum.tile([P, b - a], F32, name=f"sums{a}") for a, b in PIECES]
 
-        def multiply(g, z, codes, scales, first):
-            a, b = GROUPS[g]
+        def multiply(dst, a, b, z, codes, scales, first):
             nc.tensor.matmul_mx(
-                out=sums[g][:],
+                out=dst,
                 lhsT=w_codes[:, z, :].bitcast(FP4X4),
                 lhsT_scale=w_scales[:, z, :],
                 rhs=codes[:, a - first : b - first].bitcast(FP8X4),
@@ -168,8 +175,12 @@ def tile_picked_idxput_min_e_kernel(tc, xT, mem, w1_words, w1_scales, offs, slot
             for i, (c, d) in enumerate(PIECES):
                 if a <= c < b:
                     nc.vector.quantize_mx(out=codes1[:, c - a : d - a].bitcast(FP8X4), scales=scales1[:, c - a : d - a], in_=picked1[i][:])
-            multiply(g, 0, codes0[g], scales0[g], a)
-            multiply(g, 1, codes1, scales1, a)
+            for i, (c, d) in enumerate(PIECES):
+                if a <= c < b:
+                    width = 512 if d - c == 512 else N
+                    for e in range(c, d, width):
+                        multiply(sums[i][:, e - c : e - c + width], e, e + width, 0, codes0[g], scales0[g], a)
+                        multiply(sums[i][:, e - c : e - c + width], e, e + width, 1, codes1, scales1, a)
 
         def look_up(g):
             a, b = GROUPS[g]
@@ -182,7 +193,7 @@ def tile_picked_idxput_min_e_kernel(tc, xT, mem, w1_words, w1_scales, offs, slot
         def smaller(i):
             a, b = PIECES[i]
             g, first = divmod(a, S // 2)
-            nc.vector.tensor_tensor(new[i][:], sums[g][:, first : first + b - a], old[g][:, first : first + b - a], MIN)
+            nc.vector.tensor_tensor(new[i][:], sums[i][:], old[g][:, first : first + b - a], MIN)
 
         def put(i):
             nc.vector.tensor_copy(store[:].indirect(entries(slot_t, *PIECES[i])), new[i][:])
@@ -197,5 +208,4 @@ def tile_picked_idxput_min_e_kernel(tc, xT, mem, w1_words, w1_scales, offs, slot
         smaller(2)
         put(2)
 
-        nc.sync.dma_start(out=out[:, : U // 2], in_=store[:, : U // 2])
-        nc.scalar.dma_start(out=out[:, U // 2 :], in_=store[:, U // 2 :])
+        nc.sync.dma_start(out=out, in_=store[:])

@@ -27,7 +27,7 @@ PAIR_CHUNKS = [
     [(0, 1024, 0, 448), (1024, 2048, 672, 0)],
     [(0, 1024, 0, 512), (1024, 2048, 512, 0)],
 ]
-ROW_CHUNKS = {2: [(0, 2048, 1024)], 3: [(0, 1024, 1024), (1024, 2048, 448)]}
+ROW_CHUNKS = {2: [(0, 2048, 960)], 3: [(0, 2048, 1024)]}
 PIECES = [(0, 256), (256, 512), (512, 1024)]
 GROUPS = [(0, 512), (512, 1024)]
 
@@ -168,19 +168,16 @@ def tile_picked_idxput_min_e_kernel(tc, xT, mem, w1_words, w1_scales, offs, slot
                 in_=w1_scales[:, 4 * q : 4 * q + 4, :].rearrange("z r n -> r z n").bitcast(I32),
             )
 
-        def product(g, tag):
-            a, b = GROUPS[g]
-            codes1 = keep.tile([P, b - a], U32, name=f"codes1_{a}", tag=tag, align_bytes=64)
+        def product(i):
+            a, b = PIECES[i]
+            g = a // 512
+            codes1 = keep.tile([P, b - a], U32, name=f"codes1_{a}", tag="codes1", align_bytes=64)
             scales1 = keep.tile([P, b - a], U8, name=f"scales1_{a}", align_bytes=64)
-            for i, (c, d) in enumerate(PIECES):
-                if a <= c < b:
-                    nc.vector.quantize_mx(out=codes1[:, c - a : d - a].bitcast(FP8X4), scales=scales1[:, c - a : d - a], in_=picked1[i][:])
-            for i, (c, d) in enumerate(PIECES):
-                if a <= c < b:
-                    width = 512 if d - c == 512 else N
-                    for e in range(c, d, width):
-                        multiply(sums[i][:, e - c : e - c + width], e, e + width, 0, codes0[g], scales0[g], a)
-                        multiply(sums[i][:, e - c : e - c + width], e, e + width, 1, codes1, scales1, a)
+            nc.vector.quantize_mx(out=codes1[:].bitcast(FP8X4), scales=scales1[:], in_=picked1[i][:])
+            width = 512 if b - a == 512 else N
+            for e in range(a, b, width):
+                multiply(sums[i][:, e - a : e - a + width], e, e + width, 0, codes0[g], scales0[g], 512 * g)
+                multiply(sums[i][:, e - a : e - a + width], e, e + width, 1, codes1, scales1, a)
 
         def look_up(g):
             a, b = GROUPS[g]
@@ -198,12 +195,13 @@ def tile_picked_idxput_min_e_kernel(tc, xT, mem, w1_words, w1_scales, offs, slot
         def put(i):
             nc.vector.tensor_copy(store[:].indirect(entries(slot_t, *PIECES[i])), new[i][:])
 
-        product(0, "codes1_0")
+        product(0)
         old = [look_up(g) for g in range(len(GROUPS))]
         smaller(0)
-        smaller(1)
+        product(1)
         put(0)
-        product(1, "old0")
+        smaller(1)
+        product(2)
         put(1)
         smaller(2)
         put(2)

@@ -24,8 +24,8 @@ K_PASS = P * PACK
 
 PAIR_CHUNKS = [
     [(0, 2048, 1344, 0)],
-    [(0, 1024, 0, 448), (1024, 2048, 672, 0)],
-    [(0, 1024, 0, 512), (1024, 2048, 512, 0)],
+    [(0, 1024, 0, 448), (1024, 2048, 608, 0)],
+    [(0, 1024, 0, 576), (1024, 2048, 448, 0)],
 ]
 ROW_CHUNKS = {2: [(0, 2048, 960)], 3: [(0, 2048, 1024)]}
 PIECES = [(0, 256), (256, 512), (512, 1024)]
@@ -120,10 +120,9 @@ def tile_picked_idxput_min_e_kernel(tc, xT, mem, w1_words, w1_scales, offs, slot
 
         picked1 = [keep.tile([P, PACK * (b - a)], BF16, name=f"picked1_{a}", align_bytes=64) for a, b in PIECES]
         window = load_pair(2)
-        flat1 = keep.tile([P, PACK * 512], BF16, name="flat1", align_bytes=64)
-        for i in range(2):
-            gather_pair(picked1[i], window, 0, *PIECES[i])
-        gather_flat(flat1, window, 0, *PIECES[2])
+        flat1 = keep.tile([P, PACK * 768], BF16, name="flat1", align_bytes=64)
+        gather_pair(picked1[0], window, 0, *PIECES[0])
+        gather_flat(flat1, window, 0, 256, 1024)
 
         rows16 = keep.tile([P, 2 * T], BF16, name="rows16")
 
@@ -140,8 +139,8 @@ def tile_picked_idxput_min_e_kernel(tc, xT, mem, w1_words, w1_scales, offs, slot
 
         def gather_row(i, t, window):
             a, b = PIECES[i]
-            if i == 2:
-                dst = flat1[:, 2 * (b - a) :].rearrange("p (n e) -> p n e", e=2)[:, :, t - 2]
+            if i > 0:
+                dst = flat1[:, 2 * 768 :].rearrange("p (n e) -> p n e", e=2)[:, a - 256 : b - 256, t - 2]
             else:
                 dst = picked1[i][:].rearrange("p (n t) -> p n t", t=PACK)[:, :, t]
             if i == 0:
@@ -155,9 +154,17 @@ def tile_picked_idxput_min_e_kernel(tc, xT, mem, w1_words, w1_scales, offs, slot
         row = load_row(3)
         gather_row(0, 3, row[:])
         gather_row(1, 3, rows16[:, T:])
+        nc.gpsimd.tensor_scalar(
+            picked1[1][:].rearrange("p (n u e) -> p n u e", u=2, e=2),
+            flat1[:].rearrange("p (u n e) -> p n u e", u=2, e=2)[:, :256, :, :],
+            1.0, 0.0, MULT, ADD,
+        )
         gather_row(2, 2, rows16[:])
         gather_row(2, 3, rows16[:, T:])
-        weave(picked1[2], flat1)
+        nc.scalar.copy(
+            picked1[2][:].bitcast(U32).rearrange("p (n u) -> p n u", u=2),
+            flat1[:].bitcast(U32).rearrange("p (u n) -> p n u", u=2)[:, 256:, :],
+        )
 
         nc.sync.dma_start(slot_t[:], slot)
         nc.sync.dma_start(out=store[:], in_=mem)

@@ -15,21 +15,17 @@ FP8X4 = mybir.dt.float8_e4m3fn_x4
 FP4X4 = mybir.dt.float4_e2m1fn_x4
 COPY = mybir.ActivationFunctionType.Copy
 MIN = mybir.AluOpType.min
-MULT = mybir.AluOpType.mult
-ADD = mybir.AluOpType.add
 
 P = 128
 PACK = 4
 K_PASS = P * PACK
 
-PAIR_CHUNKS = [
-    [(0, 2048, 1344, 0)],
-    [(0, 1024, 0, 448), (1024, 2048, 608, 0)],
-    [(0, 1024, 0, 576), (1024, 2048, 448, 0)],
-]
-ROW_CHUNKS = {2: [(0, 2048, 960)], 3: [(0, 2048, 1024)]}
-PIECES = [(0, 256), (256, 512), (512, 1024)]
-GROUPS = [(0, 512), (512, 1024)]
+PIECES = [(0, 256), (256, 512), (512, 768), (768, 1024)]
+LOOKS = [(0, 512), (512, 768), (768, 1024)]
+FIRST = 768
+OWN = 256
+REST = S - OWN
+CHUNKS = [(0, 512), (512, 1024), (1024, 1536), (1536, 2048)]
 
 
 def tile_picked_idxput_min_e_kernel(tc, xT, mem, w1_words, w1_scales, offs, slot, out):
@@ -43,174 +39,126 @@ def tile_picked_idxput_min_e_kernel(tc, xT, mem, w1_words, w1_scales, offs, slot
         w_codes = keep.tile([P, 2, 2 * N], U8, name="w_codes", align_bytes=64)
         w_scales = keep.tile([P, 2, N], U8, name="w_scales", align_bytes=64)
         store = keep.tile([P, U], F32, name="store")
-
-        def x_rows(z):
-            return xT[z * K_PASS : (z + 1) * K_PASS, :].rearrange("(p t) n -> p t n", t=PACK)
+        second = keep.tile([P, U], F32, name="second")
 
         def entries(lst, a, b):
             return lst[:, a // 16 : b // 16]
 
-        def load_pair(i):
-            z, u = divmod(i, 2)
-            pair = keep.tile([P, 2 * T], BF16, name=f"pair{i}")
-            pair_v = pair[:].rearrange("p (n e) -> p n e", e=2)
-            for c0, c1, on_vector, on_gpsimd in PAIR_CHUNKS[i]:
-                if i == 1:
-                    if c0 == 0:
-                        both = keep.tile([P, 2 * T], F32, name="raw1")
-                    run = x_rows(z)[:, 2 * u : 2 * u + 2, :].rearrange("p e n -> p (e n)")
-                    first = 0 if c0 == 0 else T + c0
-                    nc.sync.dma_start(out=both[:, first : T + c1], in_=run[:, first : T + c1])
-                    turned = both[:].rearrange("p (e n) -> p n e", e=2)[:, c0:c1, :]
-                else:
-                    raw = keep.tile([P, 2, c1 - c0], F32, name=f"raw{i}_{c0}")
-                    nc.sync.dma_start(out=raw[:], in_=x_rows(z)[:, 2 * u : 2 * u + 2, c0:c1])
-                    turned = raw[:].rearrange("p e n -> p n e")
-                if i == 0 and c0 == 0:
-                    nc.sync.dma_start(offs_t[:], offs)
-                end = c1 - c0 - on_vector
-                cut = end - on_gpsimd
-                if cut:
-                    nc.scalar.activation(pair_v[:, c0 : c0 + cut, :], turned[:, :cut, :], COPY)
-                if on_gpsimd:
-                    nc.gpsimd.tensor_scalar(pair_v[:, c0 + cut : c0 + end, :], turned[:, cut:end, :], 1.0, 0.0, MULT, ADD)
-                if on_vector:
-                    nc.vector.tensor_copy(pair_v[:, c0 + end : c1, :], turned[:, end:, :])
-            return pair[:].bitcast(U32)
+        def load_row(z, t):
+            row = keep.tile([P, T], F32, name=f"row{z}_{t}")
+            rows = xT[z * K_PASS : (z + 1) * K_PASS, :].rearrange("(p t) n -> p t n", t=PACK)
+            nc.sync.dma_start(out=row[:], in_=rows[:, t, :])
+            return row
 
-        def gather_pair(dst, window, u, a, b):
-            words = dst[:].bitcast(U32).rearrange("p (n u) -> p n u", u=2)
-            nc.vector.tensor_copy(words[:, :, u], window.indirect(entries(offs_t, a, b)))
+        def quads(ap):
+            return ap.rearrange("p (n t) -> p n t", t=PACK)
 
-        def gather_flat(dst, window, u, a, b):
-            words = dst[:].bitcast(U32)
-            nc.vector.tensor_copy(words[:, u * (b - a) : (u + 1) * (b - a)], window.indirect(entries(offs_t, a, b)))
+        def gather_own(dst, t, row):
+            nc.vector.tensor_copy(quads(dst)[:, :, t], row[:].indirect(entries(offs_t, 0, OWN)))
 
-        def weave(dst, src):
-            words = dst[:].bitcast(U32).rearrange("p (n u) -> p n u", u=2)
-            nc.scalar.copy(words, src[:].bitcast(U32).rearrange("p (u n) -> p n u", u=2))
+        def gather_rest(dst, row, a, b):
+            nc.scalar.activation(dst, row[:].indirect(entries(offs_t, a, b)), COPY)
 
-        sums = [psum.tile([P, b - a], F32, name=f"sums{a}") for a, b in PIECES]
+        nc.vector.memset(w_scales[:].rearrange("p z n -> p (z n)").bitcast(I32), 0)
 
-        def multiply(dst, a, b, z, codes, scales, first):
+        sums = [psum.tile([P, b - a], F32, name=f"sums{a}") for a, b in LOOKS]
+
+        def multiply(dst, z, codes, scales, start, stop):
             nc.tensor.matmul_mx(
                 out=dst,
                 lhsT=w_codes[:, z, :].bitcast(FP4X4),
                 lhsT_scale=w_scales[:, z, :],
-                rhs=codes[:, a - first : b - first].bitcast(FP8X4),
-                rhs_scale=scales[:, a - first : b - first],
-                start=(z == 0),
-                stop=(z == 1),
+                rhs=codes.bitcast(FP8X4),
+                rhs_scale=scales,
+                start=start,
+                stop=stop,
             )
 
-        picked0 = [keep.tile([P, PACK * (b - a)], BF16, name=f"picked0_{a}", align_bytes=64) for a, b in GROUPS]
-        flat0 = keep.tile([P, PACK * 512], BF16, name="flat0", tag="flat0", align_bytes=64)
-        scales0 = [keep.tile([P, b - a], U8, name=f"scales0_{a}", align_bytes=64) for a, b in GROUPS]
-        window = load_pair(0)
-        gather_flat(flat0, window, 0, *GROUPS[1])
-        gather_pair(picked0[0], window, 0, *GROUPS[0])
-        nc.vector.memset(w_scales[:].rearrange("p z n -> p (z n)").bitcast(I32), 0)
-        window = load_pair(1)
-        gather_flat(flat0, window, 1, *GROUPS[1])
-        gather_pair(picked0[0], window, 1, *GROUPS[0])
-        weave(picked0[1], flat0)
-        codes0 = [keep.tile([P, 512], U32, name=f"codes0_{g}", tag=tag, align_bytes=64) for g, tag in enumerate(("flat0", "codes0_1"))]
-        for g in (1, 0):
-            nc.vector.quantize_mx(out=codes0[g][:].bitcast(FP8X4), scales=scales0[g][:], in_=picked0[g][:])
+        picked0 = keep.tile([P, PACK * S], BF16, name="picked0", align_bytes=64)
+        flat0 = keep.tile([P, PACK * REST], BF16, name="flat0", align_bytes=64)
+        codes0 = keep.tile([P, S], U32, name="codes0", align_bytes=64)
+        scales0 = keep.tile([P, S], U8, name="scales0", align_bytes=64)
+        for t in range(PACK):
+            row = load_row(0, t)
+            if t == 0:
+                nc.sync.dma_start(offs_t[:], offs)
+                nc.sync.dma_start(out=w_codes[:].bitcast(I32), in_=w1_words.rearrange("z p c -> p z c").bitcast(I32))
+                for q in range(4):
+                    nc.sync.dma_start(
+                        out=w_scales[32 * q : 32 * q + 4, :, :].bitcast(I32),
+                        in_=w1_scales[:, 4 * q : 4 * q + 4, :].rearrange("z r n -> r z n").bitcast(I32),
+                    )
+            gather_own(picked0[:, : PACK * OWN], t, row)
+            if t == 0:
+                nc.vector.tensor_copy(flat0[:, : FIRST - OWN], row[:].indirect(entries(offs_t, OWN, FIRST)))
+                gather_rest(flat0[:, FIRST - OWN : REST], row, FIRST, S)
+            else:
+                gather_rest(flat0[:, t * REST : (t + 1) * REST], row, OWN, S)
+        nc.vector.tensor_copy(quads(picked0[:, PACK * OWN :]), flat0[:].rearrange("p (t n) -> p n t", t=PACK))
 
         picked1 = [keep.tile([P, PACK * (b - a)], BF16, name=f"picked1_{a}", align_bytes=64) for a, b in PIECES]
-        window = load_pair(2)
-        flat1 = keep.tile([P, PACK * 768], BF16, name="flat1", align_bytes=64)
-        gather_pair(picked1[0], window, 0, *PIECES[0])
-        gather_flat(flat1, window, 0, 256, 1024)
+        flat1 = [keep.tile([P, 2 * REST], BF16, name=f"flat1_{u}", align_bytes=64) for u in range(2)]
 
-        rows16 = keep.tile([P, 2 * T], BF16, name="rows16")
-
-        def load_row(t):
-            row = keep.tile([P, T], F32, name=f"row{t}")
-            for c0, c1, on_gpsimd in ROW_CHUNKS[t]:
-                nc.sync.dma_start(out=row[:, c0:c1], in_=x_rows(1)[:, t, c0:c1])
-                cut = c1 - on_gpsimd
-                base = (t - 2) * T
-                if cut > c0:
-                    nc.scalar.activation(rows16[:, base + c0 : base + cut], row[:, c0:cut], COPY)
-                nc.gpsimd.tensor_scalar(rows16[:, base + cut : base + c1], row[:, cut:c1], 1.0, 0.0, MULT, ADD)
-            return row
-
-        def gather_row(i, t, window):
+        def weave(i, u):
             a, b = PIECES[i]
-            if i > 0:
-                dst = flat1[:, 2 * 768 :].rearrange("p (n e) -> p n e", e=2)[:, a - 256 : b - 256, t - 2]
-            else:
-                dst = picked1[i][:].rearrange("p (n t) -> p n t", t=PACK)[:, :, t]
-            if i == 0:
-                nc.vector.tensor_copy(dst, window.indirect(entries(offs_t, a, b)))
-            else:
-                nc.scalar.activation(dst, window.indirect(entries(offs_t, a, b)), COPY)
+            src = flat1[u][:].rearrange("p (e n) -> p n e", e=2)[:, a - OWN : b - OWN, :]
+            nc.vector.tensor_copy(quads(picked1[i][:])[:, :, 2 * u : 2 * u + 2], src)
 
-        row = load_row(2)
-        gather_row(0, 2, row[:])
-        gather_row(1, 2, rows16[:, :T])
-        row = load_row(3)
-        gather_row(0, 3, row[:])
-        gather_row(1, 3, rows16[:, T:])
-        nc.gpsimd.tensor_scalar(
-            picked1[1][:].rearrange("p (n u e) -> p n u e", u=2, e=2),
-            flat1[:].rearrange("p (u n e) -> p n u e", u=2, e=2)[:, :256, :, :],
-            1.0, 0.0, MULT, ADD,
-        )
-        gather_row(2, 2, rows16[:])
-        gather_row(2, 3, rows16[:, T:])
-        nc.scalar.copy(
-            picked1[2][:].bitcast(U32).rearrange("p (n u) -> p n u", u=2),
-            flat1[:].bitcast(U32).rearrange("p (u n) -> p n u", u=2)[:, 256:, :],
-        )
+        for t in range(PACK):
+            row = load_row(1, t)
+            u, e = divmod(t, 2)
+            gather_own(picked1[0][:], t, row)
+            if t < PACK - 1:
+                gather_rest(flat1[u][:, e * REST : (e + 1) * REST], row, OWN, S)
+            else:
+                for a, b in PIECES[1:]:
+                    gather_rest(flat1[u][:, e * REST + a - OWN : e * REST + b - OWN], row, a, b)
+            if t == 0:
+                nc.vector.quantize_mx(out=codes0[:].bitcast(FP8X4), scales=scales0[:], in_=picked0[:])
+                for h, (a, b) in enumerate(LOOKS):
+                    multiply(sums[h][:], 0, codes0[:, a:b], scales0[:, a:b], True, False)
+            if t == 1:
+                for i in range(1, len(PIECES)):
+                    weave(i, 0)
 
         nc.sync.dma_start(slot_t[:], slot)
         nc.sync.dma_start(out=store[:], in_=mem)
-        nc.sync.dma_start(out=w_codes[:].bitcast(I32), in_=w1_words.rearrange("z p c -> p z c").bitcast(I32))
-        for q in range(4):
-            nc.sync.dma_start(
-                out=w_scales[32 * q : 32 * q + 4, :, :].bitcast(I32),
-                in_=w1_scales[:, 4 * q : 4 * q + 4, :].rearrange("z r n -> r z n").bitcast(I32),
-            )
+        nc.sync.dma_start(out=second[:], in_=mem)
+
+        old = [keep.tile([P, b - a], F32, name=f"old{a}") for a, b in LOOKS]
+        new = [keep.tile([P, b - a], F32, name=f"new{a}") for a, b in LOOKS]
 
         def product(i):
             a, b = PIECES[i]
-            g = a // 512
-            codes1 = keep.tile([P, b - a], U32, name=f"codes1_{a}", tag="codes1", align_bytes=64)
+            h = max(i - 1, 0)
+            first = a - LOOKS[h][0]
+            codes1 = keep.tile([P, b - a], U32, name=f"codes1_{a}", align_bytes=64)
             scales1 = keep.tile([P, b - a], U8, name=f"scales1_{a}", align_bytes=64)
             nc.vector.quantize_mx(out=codes1[:].bitcast(FP8X4), scales=scales1[:], in_=picked1[i][:])
-            width = 512 if b - a == 512 else N
-            for e in range(a, b, width):
-                multiply(sums[i][:, e - a : e - a + width], e, e + width, 0, codes0[g], scales0[g], 512 * g)
-                multiply(sums[i][:, e - a : e - a + width], e, e + width, 1, codes1, scales1, a)
+            multiply(sums[h][:, first : first + b - a], 1, codes1[:], scales1[:], False, b == LOOKS[h][1])
 
-        def look_up(g):
-            a, b = GROUPS[g]
-            old = keep.tile([P, b - a], F32, name=f"old{g}", tag=f"old{g}", align_bytes=64)
-            nc.vector.tensor_copy(old[:], store[:].indirect(entries(slot_t, a, b)))
-            return old
-
-        new = [keep.tile([P, b - a], F32, name=f"new{a}") for a, b in PIECES]
+        def look_up(i):
+            nc.scalar.activation(old[i][:], store[:].indirect(entries(slot_t, *LOOKS[i])), COPY)
 
         def smaller(i):
-            a, b = PIECES[i]
-            g, first = divmod(a, S // 2)
-            nc.vector.tensor_tensor(new[i][:], sums[i][:], old[g][:, first : first + b - a], MIN)
+            nc.vector.tensor_tensor(new[i][:], sums[i][:], old[i][:], MIN)
 
-        def put(i):
-            nc.vector.tensor_copy(store[:].indirect(entries(slot_t, *PIECES[i])), new[i][:])
-
+        weave(1, 1)
         product(0)
-        old = [look_up(g) for g in range(len(GROUPS))]
-        smaller(0)
+        weave(2, 1)
         product(1)
-        put(0)
-        smaller(1)
+        weave(3, 1)
         product(2)
-        put(1)
-        smaller(2)
-        put(2)
+        product(3)
+        for i in range(len(LOOKS)):
+            look_up(i)
+        for i in range(len(LOOKS)):
+            smaller(i)
+        for i in (1, 2):
+            nc.scalar.activation(store[:].indirect(entries(slot_t, *LOOKS[i])), new[i][:], COPY)
+        nc.vector.tensor_copy(second[:].indirect(entries(slot_t, *LOOKS[0])), new[0][:])
 
-        nc.sync.dma_start(out=out, in_=store[:])
+        for c0, c1 in CHUNKS:
+            merged = keep.tile([P, c1 - c0], F32, name=f"merged{c0}")
+            nc.vector.tensor_tensor(merged[:], store[:, c0:c1], second[:, c0:c1], MIN)
+            nc.sync.dma_start(out=out[:, c0:c1], in_=merged[:])

@@ -22,6 +22,8 @@ K_PASS = P * PACK
 
 PIECES = [(0, 256), (256, 512), (512, 768), (768, 1024)]
 LOOKS = [(0, 512), (512, 768), (768, 1024)]
+SCALAR_PUTS = [(0, 288), (768, 1024)]
+VECTOR_PUT = (288, 768)
 FIRST = 768
 OWN = 256
 REST = S - OWN
@@ -82,9 +84,9 @@ def tile_picked_idxput_min_e_kernel(tc, xT, mem, w1_words, w1_scales, offs, slot
             row = load_row(0, t)
             if t == 0:
                 nc.sync.dma_start(offs_t[:], offs)
-                nc.sync.dma_start(out=w_codes[:].bitcast(I32), in_=w1_words.rearrange("z p c -> p z c").bitcast(I32))
+                nc.scalar.dma_start(out=w_codes[:].bitcast(I32), in_=w1_words.rearrange("z p c -> p z c").bitcast(I32))
                 for q in range(4):
-                    nc.sync.dma_start(
+                    nc.scalar.dma_start(
                         out=w_scales[32 * q : 32 * q + 4, :, :].bitcast(I32),
                         in_=w1_scales[:, 4 * q : 4 * q + 4, :].rearrange("z r n -> r z n").bitcast(I32),
                     )
@@ -94,7 +96,9 @@ def tile_picked_idxput_min_e_kernel(tc, xT, mem, w1_words, w1_scales, offs, slot
                 gather_rest(flat0[:, FIRST - OWN : REST], row, FIRST, S)
             else:
                 gather_rest(flat0[:, t * REST : (t + 1) * REST], row, OWN, S)
-        nc.vector.tensor_copy(quads(picked0[:, PACK * OWN :]), flat0[:].rearrange("p (t n) -> p n t", t=PACK))
+            if t % 2 == 1:
+                src = flat0[:, (t - 1) * REST : (t + 1) * REST].rearrange("p (e n) -> p n e", e=2)
+                nc.vector.tensor_copy(quads(picked0[:, PACK * OWN :])[:, :, t - 1 : t + 1], src)
 
         picked1 = [keep.tile([P, PACK * (b - a)], BF16, name=f"picked1_{a}", align_bytes=64) for a, b in PIECES]
         flat1 = [keep.tile([P, 2 * REST], BF16, name=f"flat1_{u}", align_bytes=64) for u in range(2)]
@@ -126,7 +130,7 @@ def tile_picked_idxput_min_e_kernel(tc, xT, mem, w1_words, w1_scales, offs, slot
         nc.sync.dma_start(out=second[:], in_=mem)
 
         old = [keep.tile([P, b - a], F32, name=f"old{a}") for a, b in LOOKS]
-        new = [keep.tile([P, b - a], F32, name=f"new{a}") for a, b in LOOKS]
+        new = keep.tile([P, S], F32, name="new")
 
         def product(i):
             a, b = PIECES[i]
@@ -141,7 +145,8 @@ def tile_picked_idxput_min_e_kernel(tc, xT, mem, w1_words, w1_scales, offs, slot
             nc.scalar.activation(old[i][:], store[:].indirect(entries(slot_t, *LOOKS[i])), COPY)
 
         def smaller(i):
-            nc.vector.tensor_tensor(new[i][:], sums[i][:], old[i][:], MIN)
+            a, b = LOOKS[i]
+            nc.vector.tensor_tensor(new[:, a:b], sums[i][:], old[i][:], MIN)
 
         weave(1, 1)
         product(0)
@@ -154,11 +159,13 @@ def tile_picked_idxput_min_e_kernel(tc, xT, mem, w1_words, w1_scales, offs, slot
             look_up(i)
         for i in range(len(LOOKS)):
             smaller(i)
-        for i in (1, 2):
-            nc.scalar.activation(store[:].indirect(entries(slot_t, *LOOKS[i])), new[i][:], COPY)
-        nc.vector.tensor_copy(second[:].indirect(entries(slot_t, *LOOKS[0])), new[0][:])
+        for a, b in SCALAR_PUTS:
+            nc.scalar.activation(second[:].indirect(entries(slot_t, a, b)), new[:, a:b], COPY)
+        a, b = VECTOR_PUT
+        nc.vector.tensor_copy(store[:].indirect(entries(slot_t, a, b)), new[:, a:b])
 
-        for c0, c1 in CHUNKS:
+        for j, (c0, c1) in enumerate(CHUNKS):
             merged = keep.tile([P, c1 - c0], F32, name=f"merged{c0}")
             nc.vector.tensor_tensor(merged[:], store[:, c0:c1], second[:, c0:c1], MIN)
-            nc.sync.dma_start(out=out[:, c0:c1], in_=merged[:])
+            queue = nc.scalar if j % 2 else nc.sync
+            queue.dma_start(out=out[:, c0:c1], in_=merged[:])

@@ -27,7 +27,7 @@ VECTOR_PUT = (288, 768)
 FIRST = 768
 OWN = 256
 REST = S - OWN
-CHUNKS = [(0, 512), (512, 1024), (1024, 1536), (1536, 2048)]
+CHUNKS = [(0, 256), (256, 576), (576, 896), (896, 1216), (1216, 1536), (1536, 1792), (1792, 2048)]
 
 
 def tile_picked_idxput_min_e_kernel(tc, xT, mem, w1_words, w1_scales, offs, slot, out):
@@ -112,7 +112,7 @@ def tile_picked_idxput_min_e_kernel(tc, xT, mem, w1_words, w1_scales, offs, slot
             row = load_row(1, t)
             u, e = divmod(t, 2)
             gather_own(picked1[0][:], t, row)
-            if t < PACK - 1:
+            if e == 0:
                 gather_rest(flat1[u][:, e * REST : (e + 1) * REST], row, OWN, S)
             else:
                 for a, b in PIECES[1:]:

@@ -19,14 +19,12 @@ MIN = mybir.AluOpType.min
 P = 128
 PACK = 4
 K_PASS = P * PACK
-
-PIECES = [(0, 256), (256, 512), (512, 768), (768, 1024)]
-LOOKS = [(0, 512), (512, 768), (768, 1024)]
-SCALAR_PUTS = [(0, 288), (768, 1024)]
-VECTOR_PUT = (288, 768)
-FIRST = 768
-OWN = 256
-REST = S - OWN
+Q = S // 4
+EARLY_OWN = 384
+GROUPS = [(0, Q), (Q, 3 * Q), (3 * Q, S)]
+SCALAR_WEAVE = (640, 768)
+SCALAR_PUTS = [(0, Q), (736, S)]
+VECTOR_PUT = (Q, 736)
 CHUNKS = [(0, 256), (256, 576), (576, 896), (896, 1216), (1216, 1536), (1536, 1792), (1792, 2048)]
 
 
@@ -42,6 +40,11 @@ def tile_picked_idxput_min_e_kernel(tc, xT, mem, w1_words, w1_scales, offs, slot
         w_scales = keep.tile([P, 2, N], U8, name="w_scales", align_bytes=64)
         store = keep.tile([P, U], F32, name="store")
         second = keep.tile([P, U], F32, name="second")
+        picked = [keep.tile([P, PACK * S], BF16, name=f"picked{z}", align_bytes=64) for z in range(2)]
+        codes = [keep.tile([P, S], U32, name=f"codes{z}", align_bytes=64) for z in range(2)]
+        scales = [keep.tile([P, S], U8, name=f"scales{z}", align_bytes=64) for z in range(2)]
+        sums = [psum.tile([P, b - a], F32, name=f"sums{a}") for a, b in GROUPS]
+        new = keep.tile([P, S], F32, name="new")
 
         def entries(lst, a, b):
             return lst[:, a // 16 : b // 16]
@@ -52,117 +55,92 @@ def tile_picked_idxput_min_e_kernel(tc, xT, mem, w1_words, w1_scales, offs, slot
             nc.sync.dma_start(out=row[:], in_=rows[:, t, :])
             return row
 
-        def quads(ap):
-            return ap.rearrange("p (n t) -> p n t", t=PACK)
+        def placed(z, a, b):
+            return picked[z][:, PACK * a : PACK * b].rearrange("p (n t) -> p n t", t=PACK)
 
-        def gather_own(dst, t, row):
-            nc.vector.tensor_copy(quads(dst)[:, :, t], row[:].indirect(entries(offs_t, 0, OWN)))
+        def gather_in_place(z, t, row, a, b):
+            nc.vector.tensor_copy(placed(z, a, b)[:, :, t], row[:].indirect(entries(offs_t, a, b)))
 
-        def gather_rest(dst, row, a, b):
-            nc.scalar.activation(dst, row[:].indirect(entries(offs_t, a, b)), COPY)
+        def gather_flat(flat, e, row, a, b):
+            nc.scalar.activation(flat[:, e * S + a : e * S + b], row[:].indirect(entries(offs_t, a, b)), COPY)
+
+        def weave(copy, z, u, flat, a, b):
+            src = flat[:].rearrange("p (e n) -> p n e", e=2)[:, a:b, :]
+            copy(placed(z, a, b)[:, :, 2 * u : 2 * u + 2], src)
+
+        def quantise(z, a, b):
+            nc.vector.quantize_mx(out=codes[z][:, a:b].bitcast(FP8X4), scales=scales[z][:, a:b], in_=picked[z][:, PACK * a : PACK * b])
+
+        def multiply(z, g, a, b):
+            first, last = GROUPS[g]
+            nc.tensor.matmul_mx(
+                out=sums[g][:, a - first : b - first],
+                lhsT=w_codes[:, z, :].bitcast(FP4X4),
+                lhsT_scale=w_scales[:, z, :],
+                rhs=codes[z][:, a:b].bitcast(FP8X4),
+                rhs_scale=scales[z][:, a:b],
+                start=(z == 0),
+                stop=(z == 1 and b == last),
+            )
 
         nc.vector.memset(w_scales[:].rearrange("p z n -> p (z n)").bitcast(I32), 0)
 
-        sums = [psum.tile([P, b - a], F32, name=f"sums{a}") for a, b in LOOKS]
+        for z, u in [(0, 0), (0, 1), (1, 0)]:
+            flat = keep.tile([P, 2 * S], BF16, name=f"flat{z}_{u}", align_bytes=64)
+            for e in range(2):
+                row = load_row(z, 2 * u + e)
+                if (z, u, e) == (0, 0, 0):
+                    nc.sync.dma_start(offs_t[:], offs)
+                    nc.scalar.dma_start(out=w_codes[:].bitcast(I32), in_=w1_words.rearrange("z p c -> p z c").bitcast(I32))
+                    for q in range(4):
+                        nc.scalar.dma_start(
+                            out=w_scales[32 * q : 32 * q + 4, :, :].bitcast(I32),
+                            in_=w1_scales[:, 4 * q : 4 * q + 4, :].rearrange("z r n -> r z n").bitcast(I32),
+                        )
+                gather_in_place(z, 2 * u + e, row, 0, EARLY_OWN)
+                gather_flat(flat, e, row, EARLY_OWN, S)
+            weave(nc.vector.tensor_copy, z, u, flat, EARLY_OWN, S)
+            if (z, u) == (0, 1):
+                quantise(0, 0, S)
+                for g, (a, b) in enumerate(GROUPS):
+                    multiply(0, g, a, b)
 
-        def multiply(dst, z, codes, scales, start, stop):
-            nc.tensor.matmul_mx(
-                out=dst,
-                lhsT=w_codes[:, z, :].bitcast(FP4X4),
-                lhsT_scale=w_scales[:, z, :],
-                rhs=codes.bitcast(FP8X4),
-                rhs_scale=scales,
-                start=start,
-                stop=stop,
-            )
-
-        picked0 = keep.tile([P, PACK * S], BF16, name="picked0", align_bytes=64)
-        flat0 = keep.tile([P, PACK * REST], BF16, name="flat0", align_bytes=64)
-        codes0 = keep.tile([P, S], U32, name="codes0", align_bytes=64)
-        scales0 = keep.tile([P, S], U8, name="scales0", align_bytes=64)
-        for t in range(PACK):
-            row = load_row(0, t)
-            if t == 0:
-                nc.sync.dma_start(offs_t[:], offs)
-                nc.scalar.dma_start(out=w_codes[:].bitcast(I32), in_=w1_words.rearrange("z p c -> p z c").bitcast(I32))
-                for q in range(4):
-                    nc.scalar.dma_start(
-                        out=w_scales[32 * q : 32 * q + 4, :, :].bitcast(I32),
-                        in_=w1_scales[:, 4 * q : 4 * q + 4, :].rearrange("z r n -> r z n").bitcast(I32),
-                    )
-            gather_own(picked0[:, : PACK * OWN], t, row)
-            if t == 0:
-                nc.vector.tensor_copy(flat0[:, : FIRST - OWN], row[:].indirect(entries(offs_t, OWN, FIRST)))
-                gather_rest(flat0[:, FIRST - OWN : REST], row, FIRST, S)
-            else:
-                gather_rest(flat0[:, t * REST : (t + 1) * REST], row, OWN, S)
-            if t % 2 == 1:
-                src = flat0[:, (t - 1) * REST : (t + 1) * REST].rearrange("p (e n) -> p n e", e=2)
-                nc.vector.tensor_copy(quads(picked0[:, PACK * OWN :])[:, :, t - 1 : t + 1], src)
-
-        picked1 = [keep.tile([P, PACK * (b - a)], BF16, name=f"picked1_{a}", align_bytes=64) for a, b in PIECES]
-        flat1 = [keep.tile([P, 2 * REST], BF16, name=f"flat1_{u}", align_bytes=64) for u in range(2)]
-
-        def weave(i, u):
-            a, b = PIECES[i]
-            src = flat1[u][:].rearrange("p (e n) -> p n e", e=2)[:, a - OWN : b - OWN, :]
-            nc.vector.tensor_copy(quads(picked1[i][:])[:, :, 2 * u : 2 * u + 2], src)
-
-        for t in range(PACK):
-            row = load_row(1, t)
-            u, e = divmod(t, 2)
-            gather_own(picked1[0][:], t, row)
-            if e == 0:
-                gather_rest(flat1[u][:, e * REST : (e + 1) * REST], row, OWN, S)
-            else:
-                for a, b in PIECES[1:]:
-                    gather_rest(flat1[u][:, e * REST + a - OWN : e * REST + b - OWN], row, a, b)
-            if t == 0:
-                nc.vector.quantize_mx(out=codes0[:].bitcast(FP8X4), scales=scales0[:], in_=picked0[:])
-                for h, (a, b) in enumerate(LOOKS):
-                    multiply(sums[h][:], 0, codes0[:, a:b], scales0[:, a:b], True, False)
-            if t == 1:
-                for i in range(1, len(PIECES)):
-                    weave(i, 0)
-
+        flat = keep.tile([P, 2 * S], BF16, name="flat_last", align_bytes=64)
+        row = load_row(1, 2)
+        gather_in_place(1, 2, row, 0, Q)
+        gather_flat(flat, 0, row, Q, S)
+        row = load_row(1, 3)
         nc.sync.dma_start(slot_t[:], slot)
         nc.sync.dma_start(out=store[:], in_=mem)
         nc.sync.dma_start(out=second[:], in_=mem)
+        gather_in_place(1, 3, row, 0, Q)
+        for i in range(1, 4):
+            gather_flat(flat, 1, row, i * Q, (i + 1) * Q)
+        weave(nc.vector.tensor_copy, 1, 1, flat, Q, 2 * Q)
+        weave(nc.vector.tensor_copy, 1, 1, flat, 2 * Q, SCALAR_WEAVE[0])
+        weave(nc.scalar.copy, 1, 1, flat, *SCALAR_WEAVE)
+        quantise(1, 0, 2 * Q)
+        multiply(1, 0, 0, Q)
+        multiply(1, 1, Q, 2 * Q)
+        weave(nc.vector.tensor_copy, 1, 1, flat, 3 * Q, S)
+        quantise(1, 2 * Q, 3 * Q)
+        multiply(1, 1, 2 * Q, 3 * Q)
+        quantise(1, 3 * Q, S)
+        multiply(1, 2, 3 * Q, S)
 
-        old = [keep.tile([P, b - a], F32, name=f"old{a}") for a, b in LOOKS]
-        new = keep.tile([P, S], F32, name="new")
+        def looked_up(i):
+            return store[:].indirect(entries(slot_t, i * Q, (i + 1) * Q))
 
-        def product(i):
-            a, b = PIECES[i]
-            h = max(i - 1, 0)
-            first = a - LOOKS[h][0]
-            codes1 = keep.tile([P, b - a], U32, name=f"codes1_{a}", align_bytes=64)
-            scales1 = keep.tile([P, b - a], U8, name=f"scales1_{a}", align_bytes=64)
-            nc.vector.quantize_mx(out=codes1[:].bitcast(FP8X4), scales=scales1[:], in_=picked1[i][:])
-            multiply(sums[h][:, first : first + b - a], 1, codes1[:], scales1[:], False, b == LOOKS[h][1])
-
-        def look_up(i):
-            nc.scalar.activation(old[i][:], store[:].indirect(entries(slot_t, *LOOKS[i])), COPY)
-
-        def smaller(i):
-            a, b = LOOKS[i]
-            nc.vector.tensor_tensor(new[:, a:b], sums[i][:], old[i][:], MIN)
-
-        weave(1, 1)
-        product(0)
-        weave(2, 1)
-        product(1)
-        weave(3, 1)
-        product(2)
-        product(3)
-        for i in range(len(LOOKS)):
-            look_up(i)
-        for i in range(len(LOOKS)):
-            smaller(i)
+        old = keep.tile([P, S], F32, name="old")
+        for i in (0, 1, 3):
+            nc.scalar.activation(old[:, i * Q : (i + 1) * Q], looked_up(i), COPY)
+        nc.vector.tensor_copy(old[:, 2 * Q : 3 * Q], looked_up(2))
+        for g, (a, b) in enumerate(GROUPS):
+            nc.vector.tensor_tensor(new[:, a:b], sums[g][:], old[:, a:b], MIN)
         for a, b in SCALAR_PUTS:
-            nc.scalar.activation(second[:].indirect(entries(slot_t, a, b)), new[:, a:b], COPY)
+            nc.scalar.activation(store[:].indirect(entries(slot_t, a, b)), new[:, a:b], COPY)
         a, b = VECTOR_PUT
-        nc.vector.tensor_copy(store[:].indirect(entries(slot_t, a, b)), new[:, a:b])
+        nc.vector.tensor_copy(second[:].indirect(entries(slot_t, a, b)), new[:, a:b])
 
         for j, (c0, c1) in enumerate(CHUNKS):
             merged = keep.tile([P, c1 - c0], F32, name=f"merged{c0}")

@@ -20,7 +20,7 @@ P = 128
 PACK = 4
 K_PASS = P * PACK
 Q = S // 4
-EARLY_OWN = 384
+FIRST_OWN = 320
 GROUPS = [(0, Q), (Q, 3 * Q), (3 * Q, S)]
 SCALAR_WEAVE = (640, 768)
 SCALAR_PUTS = [(0, Q), (736, S)]
@@ -97,9 +97,13 @@ def tile_picked_idxput_min_e_kernel(tc, xT, mem, w1_words, w1_scales, offs, slot
                             out=w_scales[32 * q : 32 * q + 4, :, :].bitcast(I32),
                             in_=w1_scales[:, 4 * q : 4 * q + 4, :].rearrange("z r n -> r z n").bitcast(I32),
                         )
-                gather_in_place(z, 2 * u + e, row, 0, EARLY_OWN)
-                gather_flat(flat, e, row, EARLY_OWN, S)
-            weave(nc.vector.tensor_copy, z, u, flat, EARLY_OWN, S)
+                own = FIRST_OWN if z == 0 else Q
+                gather_in_place(z, 2 * u + e, row, 0, own)
+                pieces = [(i * Q, (i + 1) * Q) for i in range(1, 4)] if (z, e) == (1, 1) else [(own, S)]
+                for a, b in pieces:
+                    gather_flat(flat, e, row, a, b)
+            for a, b in pieces:
+                weave(nc.vector.tensor_copy, z, u, flat, a, b)
             if (z, u) == (0, 1):
                 quantise(0, 0, S)
                 for g, (a, b) in enumerate(GROUPS):

@@ -38,8 +38,8 @@ def tile_picked_idxput_min_e_kernel(tc, xT, mem, w1_words, w1_scales, offs, slot
         slot_t = keep.tile([P, S // 16], U16, name="slot_t")
         w_codes = keep.tile([P, 2, 2 * N], U8, name="w_codes", align_bytes=64)
         w_scales = keep.tile([P, 2, N], U8, name="w_scales", align_bytes=64)
-        store = keep.tile([P, U], F32, name="store")
-        second = keep.tile([P, U], F32, name="second")
+        store = keep.tile([P, U], F32, name="store", align_bytes=256)
+        second = keep.tile([P, U], F32, name="second", align_bytes=256)
         picked = [keep.tile([P, PACK * S], BF16, name=f"picked{z}", align_bytes=64) for z in range(2)]
         codes = [keep.tile([P, S], U32, name=f"codes{z}", align_bytes=64) for z in range(2)]
         scales = [keep.tile([P, S], U8, name=f"scales{z}", align_bytes=64) for z in range(2)]
@@ -50,7 +50,7 @@ def tile_picked_idxput_min_e_kernel(tc, xT, mem, w1_words, w1_scales, offs, slot
             return lst[:, a // 16 : b // 16]
 
         def load_row(z, t):
-            row = keep.tile([P, T], F32, name=f"row{z}_{t}")
+            row = keep.tile([P, T], F32, name=f"row{z}_{t}", align_bytes=256)
             rows = xT[z * K_PASS : (z + 1) * K_PASS, :].rearrange("(p t) n -> p t n", t=PACK)
             nc.sync.dma_start(out=row[:], in_=rows[:, t, :])
             return row
@@ -147,7 +147,7 @@ def tile_picked_idxput_min_e_kernel(tc, xT, mem, w1_words, w1_scales, offs, slot
         nc.vector.tensor_copy(second[:].indirect(entries(slot_t, a, b)), new[:, a:b])
 
         for j, (c0, c1) in enumerate(CHUNKS):
-            merged = keep.tile([P, c1 - c0], F32, name=f"merged{c0}")
+            merged = keep.tile([P, c1 - c0], F32, name=f"merged{c0}", align_bytes=256)
             nc.vector.tensor_tensor(merged[:], store[:, c0:c1], second[:, c0:c1], MIN)
             queue = nc.scalar if j % 2 else nc.sync
             queue.dma_start(out=out[:, c0:c1], in_=merged[:])

@@ -20,7 +20,7 @@ P = 128
 PACK = 4
 K_PASS = P * PACK
 Q = S // 4
-FIRST_OWN = 320
+FIRST_OWN = (512, 384)
 GROUPS = [(0, Q), (Q, 3 * Q), (3 * Q, S)]
 SCALAR_WEAVE = (640, 768)
 SCALAR_PUTS = [(0, Q), (736, S)]
@@ -97,7 +97,7 @@ def tile_picked_idxput_min_e_kernel(tc, xT, mem, w1_words, w1_scales, offs, slot
                             out=w_scales[32 * q : 32 * q + 4, :, :].bitcast(I32),
                             in_=w1_scales[:, 4 * q : 4 * q + 4, :].rearrange("z r n -> r z n").bitcast(I32),
                         )
-                own = FIRST_OWN if z == 0 else Q
+                own = FIRST_OWN[u] if z == 0 else Q
                 gather_in_place(z, 2 * u + e, row, 0, own)
                 pieces = [(i * Q, (i + 1) * Q) for i in range(1, 4)] if (z, e) == (1, 1) else [(own, S)]
                 for a, b in pieces:

@@ -22,7 +22,8 @@ K_PASS = P * PACK
 Q = S // 4
 FIRST_OWN = (512, 384)
 GROUPS = [(0, Q), (Q, 3 * Q), (3 * Q, S)]
-SCALAR_WEAVE = (640, 768)
+SCALAR_LOOKS = [(0, Q), (Q, 640), (3 * Q, S)]
+VECTOR_LOOK = (640, 3 * Q)
 SCALAR_PUTS = [(0, Q), (736, S)]
 VECTOR_PUT = (Q, 736)
 CHUNKS = [(0, 256), (256, 576), (576, 896), (896, 1216), (1216, 1536), (1536, 1792), (1792, 2048)]
@@ -121,8 +122,7 @@ def tile_picked_idxput_min_e_kernel(tc, xT, mem, w1_words, w1_scales, offs, slot
         for i in range(1, 4):
             gather_flat(flat, 1, row, i * Q, (i + 1) * Q)
         weave(nc.vector.tensor_copy, 1, 1, flat, Q, 2 * Q)
-        weave(nc.vector.tensor_copy, 1, 1, flat, 2 * Q, SCALAR_WEAVE[0])
-        weave(nc.scalar.copy, 1, 1, flat, *SCALAR_WEAVE)
+        weave(nc.vector.tensor_copy, 1, 1, flat, 2 * Q, 3 * Q)
         quantise(1, 0, 2 * Q)
         multiply(1, 0, 0, Q)
         multiply(1, 1, Q, 2 * Q)
@@ -132,13 +132,14 @@ def tile_picked_idxput_min_e_kernel(tc, xT, mem, w1_words, w1_scales, offs, slot
         quantise(1, 3 * Q, S)
         multiply(1, 2, 3 * Q, S)
 
-        def looked_up(i):
-            return store[:].indirect(entries(slot_t, i * Q, (i + 1) * Q))
+        def looked_up(a, b):
+            return store[:].indirect(entries(slot_t, a, b))
 
         old = keep.tile([P, S], F32, name="old")
-        for i in (0, 1, 3):
-            nc.scalar.activation(old[:, i * Q : (i + 1) * Q], looked_up(i), COPY)
-        nc.vector.tensor_copy(old[:, 2 * Q : 3 * Q], looked_up(2))
+        for a, b in SCALAR_LOOKS:
+            nc.scalar.activation(old[:, a:b], looked_up(a, b), COPY)
+        a, b = VECTOR_LOOK
+        nc.vector.tensor_copy(old[:, a:b], looked_up(a, b))
         for g, (a, b) in enumerate(GROUPS):
             nc.vector.tensor_tensor(new[:, a:b], sums[g][:], old[:, a:b], MIN)
         for a, b in SCALAR_PUTS:

@@ -22,6 +22,7 @@ K_PASS = P * PACK
 Q = S // 4
 FIRST_OWN = (512, 384)
 GROUPS = [(0, Q), (Q, 3 * Q), (3 * Q, S)]
+SCALAR_WEAVE = (640, 768)
 SCALAR_LOOKS = [(0, Q), (Q, 640), (3 * Q, S)]
 VECTOR_LOOK = (640, 3 * Q)
 SCALAR_PUTS = [(0, Q), (736, S)]
@@ -122,7 +123,8 @@ def tile_picked_idxput_min_e_kernel(tc, xT, mem, w1_words, w1_scales, offs, slot
         for i in range(1, 4):
             gather_flat(flat, 1, row, i * Q, (i + 1) * Q)
         weave(nc.vector.tensor_copy, 1, 1, flat, Q, 2 * Q)
-        weave(nc.vector.tensor_copy, 1, 1, flat, 2 * Q, 3 * Q)
+        weave(nc.vector.tensor_copy, 1, 1, flat, 2 * Q, SCALAR_WEAVE[0])
+        weave(nc.scalar.copy, 1, 1, flat, *SCALAR_WEAVE)
         quantise(1, 0, 2 * Q)
         multiply(1, 0, 0, Q)
         multiply(1, 1, Q, 2 * Q)
@@ -143,9 +145,9 @@ def tile_picked_idxput_min_e_kernel(tc, xT, mem, w1_words, w1_scales, offs, slot
         for g, (a, b) in enumerate(GROUPS):
             nc.vector.tensor_tensor(new[:, a:b], sums[g][:], old[:, a:b], MIN)
         for a, b in SCALAR_PUTS:
-            nc.scalar.activation(store[:].indirect(entries(slot_t, a, b)), new[:, a:b], COPY)
+            nc.scalar.activation(second[:].indirect(entries(slot_t, a, b)), new[:, a:b], COPY)
         a, b = VECTOR_PUT
-        nc.vector.tensor_copy(second[:].indirect(entries(slot_t, a, b)), new[:, a:b])
+        nc.vector.tensor_copy(store[:].indirect(entries(slot_t, a, b)), new[:, a:b])
 
         for j, (c0, c1) in enumerate(CHUNKS):
             merged = keep.tile([P, c1 - c0], F32, name=f"merged{c0}", align_bytes=256)

@@ -40,8 +40,8 @@ def tile_picked_idxput_min_e_kernel(tc, xT, mem, w1_words, w1_scales, offs, slot
         slot_t = keep.tile([P, S // 16], U16, name="slot_t")
         w_codes = keep.tile([P, 2, 2 * N], U8, name="w_codes", align_bytes=64)
         w_scales = keep.tile([P, 2, N], U8, name="w_scales", align_bytes=64)
-        store = keep.tile([P, U], F32, name="store", align_bytes=256)
-        second = keep.tile([P, U], F32, name="second", align_bytes=256)
+        store = keep.tile([P, U], F32, name="store", align_bytes=4096)
+        second = keep.tile([P, U], F32, name="second", align_bytes=4096)
         picked = [keep.tile([P, PACK * S], BF16, name=f"picked{z}", align_bytes=64) for z in range(2)]
         codes = [keep.tile([P, S], U32, name=f"codes{z}", align_bytes=64) for z in range(2)]
         scales = [keep.tile([P, S], U8, name=f"scales{z}", align_bytes=64) for z in range(2)]
@@ -52,7 +52,7 @@ def tile_picked_idxput_min_e_kernel(tc, xT, mem, w1_words, w1_scales, offs, slot
             return lst[:, a // 16 : b // 16]
 
         def load_row(z, t):
-            row = keep.tile([P, T], F32, name=f"row{z}_{t}", align_bytes=256)
+            row = keep.tile([P, T], F32, name=f"row{z}_{t}", align_bytes=4096)
             rows = xT[z * K_PASS : (z + 1) * K_PASS, :].rearrange("(p t) n -> p t n", t=PACK)
             nc.sync.dma_start(out=row[:], in_=rows[:, t, :])
             return row
@@ -150,7 +150,7 @@ def tile_picked_idxput_min_e_kernel(tc, xT, mem, w1_words, w1_scales, offs, slot
         nc.vector.tensor_copy(store[:].indirect(entries(slot_t, a, b)), new[:, a:b])
 
         for j, (c0, c1) in enumerate(CHUNKS):
-            merged = keep.tile([P, c1 - c0], F32, name=f"merged{c0}", align_bytes=256)
+            merged = keep.tile([P, c1 - c0], F32, name=f"merged{c0}", align_bytes=1024)
             nc.vector.tensor_tensor(merged[:], store[:, c0:c1], second[:, c0:c1], MIN)
             queue = nc.scalar if j % 2 else nc.sync
             queue.dma_start(out=out[:, c0:c1], in_=merged[:])

@@ -19,14 +19,15 @@ MIN = mybir.AluOpType.min
 P = 128
 PACK = 4
 K_PASS = P * PACK
-Q = S // 4
-FIRST_OWN = (512, 384)
-GROUPS = [(0, Q), (Q, 3 * Q), (3 * Q, S)]
-SCALAR_WEAVE = (640, 768)
-SCALAR_LOOKS = [(0, Q), (Q, 640), (3 * Q, S)]
-VECTOR_LOOK = (640, 3 * Q)
-SCALAR_PUTS = [(0, Q), (736, S)]
-VECTOR_PUT = (Q, 736)
+VECTOR_SHARE = (576, 448, 448, 384)
+GROUPS = [(0, 256), (256, 768), (768, S)]
+LAST_PIECES = [(384, 768), (0, 384), (768, S)]
+LAST_PRODUCTS = [[(384, 640), (640, 768)], [(0, 256), (256, 384)], [(768, S)]]
+CLOSING = (256, 384, S)
+SCALAR_LOOKS = [(0, 256), (256, 416), (768, S)]
+VECTOR_LOOK = (416, 768)
+SCALAR_PUTS = [(0, 256), (736, S)]
+VECTOR_PUT = (256, 736)
 CHUNKS = [(0, 256), (256, 576), (576, 896), (896, 1216), (1216, 1536), (1536, 1792), (1792, 2048)]
 
 
@@ -46,6 +47,7 @@ def tile_picked_idxput_min_e_kernel(tc, xT, mem, w1_words, w1_scales, offs, slot
         codes = [keep.tile([P, S], U32, name=f"codes{z}", align_bytes=64) for z in range(2)]
         scales = [keep.tile([P, S], U8, name=f"scales{z}", align_bytes=64) for z in range(2)]
         sums = [psum.tile([P, b - a], F32, name=f"sums{a}") for a, b in GROUPS]
+        old = keep.tile([P, S], F32, name="old")
         new = keep.tile([P, S], F32, name="new")
 
         def entries(lst, a, b):
@@ -57,23 +59,20 @@ def tile_picked_idxput_min_e_kernel(tc, xT, mem, w1_words, w1_scales, offs, slot
             nc.sync.dma_start(out=row[:], in_=rows[:, t, :])
             return row
 
-        def placed(z, a, b):
-            return picked[z][:, PACK * a : PACK * b].rearrange("p (n t) -> p n t", t=PACK)
+        def placed(z, t, a, b):
+            return picked[z][:, PACK * a : PACK * b].rearrange("p (n t) -> p n t", t=PACK)[:, :, t]
 
-        def gather_in_place(z, t, row, a, b):
-            nc.vector.tensor_copy(placed(z, a, b)[:, :, t], row[:].indirect(entries(offs_t, a, b)))
+        def vector_gather(z, t, row, a, b):
+            nc.vector.tensor_copy(placed(z, t, a, b), row[:].indirect(entries(offs_t, a, b)))
 
-        def gather_flat(flat, e, row, a, b):
-            nc.scalar.activation(flat[:, e * S + a : e * S + b], row[:].indirect(entries(offs_t, a, b)), COPY)
-
-        def weave(copy, z, u, flat, a, b):
-            src = flat[:].rearrange("p (e n) -> p n e", e=2)[:, a:b, :]
-            copy(placed(z, a, b)[:, :, 2 * u : 2 * u + 2], src)
+        def scalar_gather(z, t, row, a, b):
+            nc.scalar.activation(placed(z, t, a, b), row[:].indirect(entries(offs_t, a, b)), COPY)
 
         def quantise(z, a, b):
             nc.vector.quantize_mx(out=codes[z][:, a:b].bitcast(FP8X4), scales=scales[z][:, a:b], in_=picked[z][:, PACK * a : PACK * b])
 
-        def multiply(z, g, a, b):
+        def multiply(z, a, b):
+            g = [i for i, (first, last) in enumerate(GROUPS) if first <= a < last][0]
             first, last = GROUPS[g]
             nc.tensor.matmul_mx(
                 out=sums[g][:, a - first : b - first],
@@ -82,62 +81,44 @@ def tile_picked_idxput_min_e_kernel(tc, xT, mem, w1_words, w1_scales, offs, slot
                 rhs=codes[z][:, a:b].bitcast(FP8X4),
                 rhs_scale=scales[z][:, a:b],
                 start=(z == 0),
-                stop=(z == 1 and b == last),
+                stop=(z == 1 and b in CLOSING),
             )
 
         nc.vector.memset(w_scales[:].rearrange("p z n -> p (z n)").bitcast(I32), 0)
 
-        for z, u in [(0, 0), (0, 1), (1, 0)]:
-            flat = keep.tile([P, 2 * S], BF16, name=f"flat{z}_{u}", align_bytes=64)
-            for e in range(2):
-                row = load_row(z, 2 * u + e)
-                if (z, u, e) == (0, 0, 0):
-                    nc.sync.dma_start(offs_t[:], offs)
-                    nc.scalar.dma_start(out=w_codes[:].bitcast(I32), in_=w1_words.rearrange("z p c -> p z c").bitcast(I32))
-                    for q in range(4):
-                        nc.scalar.dma_start(
-                            out=w_scales[32 * q : 32 * q + 4, :, :].bitcast(I32),
-                            in_=w1_scales[:, 4 * q : 4 * q + 4, :].rearrange("z r n -> r z n").bitcast(I32),
-                        )
-                own = FIRST_OWN[u] if z == 0 else Q
-                gather_in_place(z, 2 * u + e, row, 0, own)
-                pieces = [(i * Q, (i + 1) * Q) for i in range(1, 4)] if (z, e) == (1, 1) else [(own, S)]
-                for a, b in pieces:
-                    gather_flat(flat, e, row, a, b)
-            for a, b in pieces:
-                weave(nc.vector.tensor_copy, z, u, flat, a, b)
-            if (z, u) == (0, 1):
+        for z, t in [(0, 0), (0, 1), (0, 2), (0, 3), (1, 0), (1, 1), (1, 2)]:
+            row = load_row(z, t)
+            if (z, t) == (0, 0):
+                nc.sync.dma_start(offs_t[:], offs)
+                nc.scalar.dma_start(out=w_codes[:].bitcast(I32), in_=w1_words.rearrange("z p c -> p z c").bitcast(I32))
+                for q in range(4):
+                    nc.scalar.dma_start(
+                        out=w_scales[32 * q : 32 * q + 4, :, :].bitcast(I32),
+                        in_=w1_scales[:, 4 * q : 4 * q + 4, :].rearrange("z r n -> r z n").bitcast(I32),
+                    )
+            own = VECTOR_SHARE[2 * z + t // 2]
+            vector_gather(z, t, row, 0, own)
+            scalar_gather(z, t, row, own, S)
+            if (z, t) == (0, 3):
                 quantise(0, 0, S)
-                for g, (a, b) in enumerate(GROUPS):
-                    multiply(0, g, a, b)
+                for a, b in GROUPS:
+                    multiply(0, a, b)
 
-        flat = keep.tile([P, 2 * S], BF16, name="flat_last", align_bytes=64)
-        row = load_row(1, 2)
-        gather_in_place(1, 2, row, 0, Q)
-        gather_flat(flat, 0, row, Q, S)
         row = load_row(1, 3)
         nc.sync.dma_start(slot_t[:], slot)
         nc.sync.dma_start(out=store[:], in_=mem)
         nc.sync.dma_start(out=second[:], in_=mem)
-        gather_in_place(1, 3, row, 0, Q)
-        for i in range(1, 4):
-            gather_flat(flat, 1, row, i * Q, (i + 1) * Q)
-        weave(nc.vector.tensor_copy, 1, 1, flat, Q, 2 * Q)
-        weave(nc.vector.tensor_copy, 1, 1, flat, 2 * Q, SCALAR_WEAVE[0])
-        weave(nc.scalar.copy, 1, 1, flat, *SCALAR_WEAVE)
-        quantise(1, 0, 2 * Q)
-        multiply(1, 0, 0, Q)
-        multiply(1, 1, Q, 2 * Q)
-        weave(nc.vector.tensor_copy, 1, 1, flat, 3 * Q, S)
-        quantise(1, 2 * Q, 3 * Q)
-        multiply(1, 1, 2 * Q, 3 * Q)
-        quantise(1, 3 * Q, S)
-        multiply(1, 2, 3 * Q, S)
+        vector_gather(1, 3, row, *LAST_PIECES[1])
+        for a, b in LAST_PIECES[0::2]:
+            scalar_gather(1, 3, row, a, b)
+        for (a, b), products in zip(LAST_PIECES, LAST_PRODUCTS):
+            quantise(1, a, b)
+            for c, d in products:
+                multiply(1, c, d)
 
         def looked_up(a, b):
             return store[:].indirect(entries(slot_t, a, b))
 
-        old = keep.tile([P, S], F32, name="old")
         for a, b in SCALAR_LOOKS:
             nc.scalar.activation(old[:, a:b], looked_up(a, b), COPY)
         a, b = VECTOR_LOOK
@@ -145,9 +126,9 @@ def tile_picked_idxput_min_e_kernel(tc, xT, mem, w1_words, w1_scales, offs, slot
         for g, (a, b) in enumerate(GROUPS):
             nc.vector.tensor_tensor(new[:, a:b], sums[g][:], old[:, a:b], MIN)
         for a, b in SCALAR_PUTS:
-            nc.scalar.activation(second[:].indirect(entries(slot_t, a, b)), new[:, a:b], COPY)
+            nc.scalar.activation(store[:].indirect(entries(slot_t, a, b)), new[:, a:b], COPY)
         a, b = VECTOR_PUT
-        nc.vector.tensor_copy(store[:].indirect(entries(slot_t, a, b)), new[:, a:b])
+        nc.vector.tensor_copy(second[:].indirect(entries(slot_t, a, b)), new[:, a:b])
 
         for j, (c0, c1) in enumerate(CHUNKS):
             merged = keep.tile([P, c1 - c0], F32, name=f"merged{c0}", align_bytes=1024)

@@ -130,8 +130,7 @@ def tile_picked_idxput_min_e_kernel(tc, xT, mem, w1_words, w1_scales, offs, slot
         a, b = VECTOR_PUT
         nc.vector.tensor_copy(second[:].indirect(entries(slot_t, a, b)), new[:, a:b])
 
-        for j, (c0, c1) in enumerate(CHUNKS):
+        for c0, c1 in CHUNKS:
             merged = keep.tile([P, c1 - c0], F32, name=f"merged{c0}", align_bytes=1024)
             nc.vector.tensor_tensor(merged[:], store[:, c0:c1], second[:, c0:c1], MIN)
-            queue = nc.scalar if j % 2 else nc.sync
-            queue.dma_start(out=out[:, c0:c1], in_=merged[:])
+            nc.sync.dma_start(out=out[:, c0:c1], in_=merged[:])

from contextlib import ExitStack

import concourse.mybir as mybir

K, T, S, N, U = 1024, 2048, 1024, 128, 2048
FLOPS = 2 * K * S * N

F32 = mybir.dt.float32
BF16 = mybir.dt.bfloat16
I32 = mybir.dt.int32
U32 = mybir.dt.uint32
U16 = mybir.dt.uint16
U8 = mybir.dt.uint8
FP8X4 = mybir.dt.float8_e4m3fn_x4
FP4X4 = mybir.dt.float4_e2m1fn_x4
COPY = mybir.ActivationFunctionType.Copy
MIN = mybir.AluOpType.min

P = 128
PACK = 4
K_PASS = P * PACK
VECTOR_SHARE = (576, 448, 448, 384)
GROUPS = [(0, 256), (256, 768), (768, S)]
LAST_PIECES = [(384, 768), (0, 384), (768, S)]
LAST_PRODUCTS = [[(384, 640), (640, 768)], [(0, 256), (256, 384)], [(768, S)]]
CLOSING = (256, 384, S)
SCALAR_LOOKS = [(0, 256), (256, 416), (768, S)]
VECTOR_LOOK = (416, 768)
SCALAR_PUTS = [(0, 256), (736, S)]
VECTOR_PUT = (256, 736)
CHUNKS = [(0, 256), (256, 576), (576, 896), (896, 1216), (1216, 1536), (1536, 1792), (1792, 2048)]


def tile_picked_idxput_min_e_kernel(tc, xT, mem, w1_words, w1_scales, offs, slot, out):
    nc = tc.nc
    with ExitStack() as ctx:
        keep = ctx.enter_context(tc.tile_pool(name="keep", bufs=1))
        psum = ctx.enter_context(tc.psum_pool(name="psum", bufs=1))

        offs_t = keep.tile([P, S // 16], U16, name="offs_t")
        slot_t = keep.tile([P, S // 16], U16, name="slot_t")
        w_codes = keep.tile([P, 2, 2 * N], U8, name="w_codes", align_bytes=64)
        w_scales = keep.tile([P, 2, N], U8, name="w_scales", align_bytes=64)
        store = keep.tile([P, U], F32, name="store", align_bytes=4096)
        second = keep.tile([P, U], F32, name="second", align_bytes=4096)
        picked = [keep.tile([P, PACK * S], BF16, name=f"picked{z}", align_bytes=64) for z in range(2)]
        codes = [keep.tile([P, S], U32, name=f"codes{z}", align_bytes=64) for z in range(2)]
        scales = [keep.tile([P, S], U8, name=f"scales{z}", align_bytes=64) for z in range(2)]
        sums = [psum.tile([P, b - a], F32, name=f"sums{a}") for a, b in GROUPS]
        old = keep.tile([P, S], F32, name="old")
        new = keep.tile([P, S], F32, name="new")

        def entries(lst, a, b):
            return lst[:, a // 16 : b // 16]

        def load_row(z, t):
            row = keep.tile([P, T], F32, name=f"row{z}_{t}", align_bytes=4096)
            rows = xT[z * K_PASS : (z + 1) * K_PASS, :].rearrange("(p t) n -> p t n", t=PACK)
            nc.sync.dma_start(out=row[:], in_=rows[:, t, :])
            return row

        def placed(z, t, a, b):
            return picked[z][:, PACK * a : PACK * b].rearrange("p (n t) -> p n t", t=PACK)[:, :, t]

        def vector_gather(z, t, row, a, b):
            nc.vector.tensor_copy(placed(z, t, a, b), row[:].indirect(entries(offs_t, a, b)))

        def scalar_gather(z, t, row, a, b):
            nc.scalar.activation(placed(z, t, a, b), row[:].indirect(entries(offs_t, a, b)), COPY)

        def quantise(z, a, b):
            nc.vector.quantize_mx(out=codes[z][:, a:b].bitcast(FP8X4), scales=scales[z][:, a:b], in_=picked[z][:, PACK * a : PACK * b])

        def multiply(z, a, b):
            g = [i for i, (first, last) in enumerate(GROUPS) if first <= a < last][0]
            first, last = GROUPS[g]
            nc.tensor.matmul_mx(
                out=sums[g][:, a - first : b - first],
                lhsT=w_codes[:, z, :].bitcast(FP4X4),
                lhsT_scale=w_scales[:, z, :],
                rhs=codes[z][:, a:b].bitcast(FP8X4),
                rhs_scale=scales[z][:, a:b],
                start=(z == 0),
                stop=(z == 1 and b in CLOSING),
            )

        nc.vector.memset(w_scales[:].rearrange("p z n -> p (z n)").bitcast(I32), 0)

        for z, t in [(0, 0), (0, 1), (0, 2), (0, 3), (1, 0), (1, 1), (1, 2)]:
            row = load_row(z, t)
            if (z, t) == (0, 0):
                nc.sync.dma_start(offs_t[:], offs)
                nc.scalar.dma_start(out=w_codes[:].bitcast(I32), in_=w1_words.rearrange("z p c -> p z c").bitcast(I32))
                for q in range(4):
                    nc.scalar.dma_start(
                        out=w_scales[32 * q : 32 * q + 4, :, :].bitcast(I32),
                        in_=w1_scales[:, 4 * q : 4 * q + 4, :].rearrange("z r n -> r z n").bitcast(I32),
                    )
            own = VECTOR_SHARE[2 * z + t // 2]
            vector_gather(z, t, row, 0, own)
            scalar_gather(z, t, row, own, S)
            if (z, t) == (0, 3):
                quantise(0, 0, S)
                for a, b in GROUPS:
                    multiply(0, a, b)

        row = load_row(1, 3)
        nc.sync.dma_start(slot_t[:], slot)
        nc.sync.dma_start(out=store[:], in_=mem)
        nc.sync.dma_start(out=second[:], in_=mem)
        vector_gather(1, 3, row, *LAST_PIECES[1])
        for a, b in LAST_PIECES[0::2]:
            scalar_gather(1, 3, row, a, b)
        for (a, b), products in zip(LAST_PIECES, LAST_PRODUCTS):
            quantise(1, a, b)
            for c, d in products:
                multiply(1, c, d)

        def looked_up(a, b):
            return store[:].indirect(entries(slot_t, a, b))

        for a, b in SCALAR_LOOKS:
            nc.scalar.activation(old[:, a:b], looked_up(a, b), COPY)
        a, b = VECTOR_LOOK
        nc.vector.tensor_copy(old[:, a:b], looked_up(a, b))
        for g, (a, b) in enumerate(GROUPS):
            nc.vector.tensor_tensor(new[:, a:b], sums[g][:], old[:, a:b], MIN)
        for a, b in SCALAR_PUTS:
            nc.scalar.activation(store[:].indirect(entries(slot_t, a, b)), new[:, a:b], COPY)
        a, b = VECTOR_PUT
        nc.vector.tensor_copy(second[:].indirect(entries(slot_t, a, b)), new[:, a:b])

        for c0, c1 in CHUNKS:
            merged = keep.tile([P, c1 - c0], F32, name=f"merged{c0}", align_bytes=1024)
            nc.vector.tensor_tensor(merged[:], store[:, c0:c1], second[:, c0:c1], MIN)
            nc.sync.dma_start(out=out[:, c0:c1], in_=merged[:])
